import numpy as np, ml_dtypes
CORES = [3,7,11,15,131,135,139,143]
N = 8
import mx_ref
BF = ml_dtypes.bfloat16
def gentries(a):
    return np.ascontiguousarray(a.reshape(8, 16, -1).transpose(0, 2, 1)).reshape(8, -1)
def gtable(e):
    e = np.asarray(e); return np.ascontiguousarray(e.reshape(8, -1, 16).transpose(0, 2, 1)).reshape(128, -1).astype(np.int32)
def gcols(t, e):
    v = np.concatenate([t.reshape(8, 16, -1, 4), np.zeros((8, 16, 1, 4), BF)], axis=2)
    return np.ascontiguousarray(np.stack([v[g][:, e[g]] for g in range(8)])).reshape(128, -1)
def tile(rs):
    return np.stack(rs, axis=2).reshape(128, -1).astype(BF)
def pick(q, e):
    c = np.concatenate([q[0].reshape(128, -1, 4), np.zeros((128, 1, 4), np.uint8)], axis=1); s = np.concatenate([q[1], np.ones((16, 1), np.uint8)], axis=1)
    return (np.ascontiguousarray(c[:, e].reshape(128, -1)), np.ascontiguousarray(s[:, e]))
def join(*qs):
    return (np.concatenate([q[0] for q in qs], axis=1), np.concatenate([q[1] for q in qs], axis=1))
def put(q, e, v):
    c, s = q[0].reshape(128, -1, 4).copy(), q[1].copy(); c[:, e] = v[0].reshape(128, -1, 4); s[:, e] = v[1]
    return (c.reshape(128, -1), s)
def pk(c, s):
    return (np.ascontiguousarray(c), mx_ref.live(s))
def emit(q):
    return q[0], q[1]
def packed(v, rng):
    q = [mx_ref.quantize(np.ascontiguousarray(v[r])) for r in range(N)]
    return np.stack([a for a, b in q]), np.stack([mx_ref.plane(b, rng) for a, b in q])
def values_of_codes():
    e, c = np.zeros((128, 128, 4), np.float32), np.zeros((128, 2, 4), np.uint8)
    e[np.arange(128), np.arange(128), 0] = 1
    c[:127, :, 0] = np.arange(256).reshape(2, 128).T[:127]
    return mx_ref.matmul(mx_ref.quantize(e.reshape(128, 512).astype(BF)), (c.reshape(128, 8), np.full((16, 2), 127, np.uint8))).T.reshape(-1).astype(np.float64)
CODE_VALUE, SCALE_VALUE = values_of_codes(), 2.0 ** (np.arange(256) - 127.0)
def decode(q):
    return (CODE_VALUE[q[0]].reshape(16, 8, -1, 4) * SCALE_VALUE[q[1]][:, None, :, None] + 0.0).reshape(128, -1).astype(np.float32)
def f(rng, *shape):
    return mx_ref.flush((rng.standard_normal(shape, dtype=np.float32) * np.exp2(rng.integers(-2, 3, shape[:-1] + (1,)))).astype(BF))
def wide(rng, *shape, cols=0):
    v = rng.standard_normal(shape, dtype=np.float32) * np.exp2(rng.integers(-12, 13, shape)).astype(np.float32)
    if cols: v *= np.repeat(np.exp2(rng.integers(-cols, cols + 1, shape[:-2] + (1, shape[-1] // 4))) * (rng.random(shape[:-2] + (1, shape[-1] // 4)) > 0.0625), 4, axis=-1).astype(np.float32)
    return mx_ref.flush(v.astype(BF))
C = 288
STEP = [2, 4, 1]
GAPS = [[2, 4, 5, 6, 7, 8], [3, 4, 5, 6, 7, 8]]
def numbers_of(rng):
    return {"x": np.array(f(rng, N, 128, 4 * C)), "u": np.array(f(rng, N, 128, 512)), "v": np.array(f(rng, N, 128, 512))}
def full(rng, k):
    h = 128 + rng.permutation(128)[:k]
    low = rng.permutation(np.concatenate([2 * h, 2 * h + 1]))[:C - 127 - k]
    return np.sort(np.concatenate([np.arange(1, 128), h, low]))
def below(h):
    return np.concatenate([np.arange(h << n, (h + 1) << n) for n in range(10 - h.bit_length())])
def lean(side, slot):
    c = 3 - side
    return np.sort(np.concatenate([[1], below(2 + side), np.concatenate([[c], below(2 * c + slot)])[:C - 256]]))
def ragged(rng, first):
    cuts, left = [], 511 - C
    for n, most in [(n, 1) for n in first] + [(n, 9) for n in range(3, 9)]:
        size = 2 ** (9 - n) - 1
        k = min(most, left // size)
        cuts += [n] * k
        left -= k * size
    keep = np.arange(512) > 0
    for n in sorted(cuts):
        h = np.arange(2 ** n, 2 ** (n + 1))
        h = int(rng.choice(h[keep[h] & keep[h ^ 1]]))
        keep[below(h)] = False
    return np.flatnonzero(keep)
def grown(h, places):
    at = np.zeros(512, np.int64)
    at[h] = places
    e = np.zeros(C, np.int64)
    e[places[1:]] = 2 * at[h[1:] >> 1] + (h[1:] & 1)
    return e
def shuffled(rng):
    return np.concatenate([[0], 1 + rng.permutation(C - 1)])
def trees(rng):
    t = np.stack([np.stack([grown(full(rng, int(rng.integers(112, 129))), shuffled(rng)) for g in range(8)]) for r in range(N)])
    o = rng.permutation(8)
    for r in range(N):
        for n in range(2): t[r, o[(r + 4 * n) % 8]] = grown(ragged(rng, GAPS[n]), shuffled(rng))
    return t
def stored(t):
    return {"se": np.stack([gtable(t[r]) for r in range(N)])}
def weights(rng, w):
    c, s = packed(np.ascontiguousarray(w).reshape(N, 128, 2048), rng)
    return {"wc": c, "ws": s}
def layers(rng, still=[], pairs=False):
    w = np.array(f(rng, N, 128, 2048)).reshape(N, 8, 16, 4, 8, 16, 4)
    for i in still:
        w[:, :, i] = 0
        w[:, :, :, :, :, i] = 0
    if pairs:
        w[:, :, :, :, :, 8:] = 0
        for g in range(8):
            w[:, g, 8, 0, g, 8, 0] = -28.0
            for b in range(4): w[:, g, 10, b, g, 9, 0] = -2.0 ** (b - 5)
    return weights(rng, w)
def setup_inputs(rng):
    return {**numbers_of(rng), **stored(trees(rng)), **layers(rng)}
def setup_inputs_ties(rng):
    d = numbers_of(rng)
    o = rng.permutation(N)
    k = rng.integers(-1, 2, (N, 8, C)).astype(np.float32)
    k[o[1]] = -1
    x = d["x"].reshape(N, 8, 16, C, 4)
    x[:, :, 0] = 0
    x[:, :, 0, :, 0] = k.astype(BF)
    a = np.exp2(rng.integers(-3, 4, (1, 8, 1)).astype(np.float32))
    x[:, :, 8:] = 0
    x[:, :, 8, :, 0] = (-1.125 * a).astype(BF)
    x[:, :, 10, :, 0] = (-0.0703125 * a).astype(BF)
    c = np.ones(N, np.float32)
    c[o[0]] = 0
    c[o[2]] = -1
    u = d["u"].reshape(N, 128, 128, 4)
    u[:, :, ::16] = 0
    for h in range(0, 128, 16): u[:, h, h, 0] = c.astype(BF)
    return {"x": x.reshape(N, 128, 4 * C), "u": u.reshape(N, 128, 512), "v": d["v"], **stored(trees(rng)), **layers(rng, [0], True)}
def setup_inputs_near(rng):
    d = numbers_of(rng)
    o = rng.permutation(N) % 2
    k = np.where(o == 0, 2.0 ** -30, 1.0).astype(np.float32)
    x = np.zeros((N, 8, 16, C, 4), np.float32)
    s = rng.integers(-1, 2, (N, 8, C)) * k[:, None, None]
    x[:, :, 0, :, 0] = 1.125 * s
    x[:, :, 1, :, 0] = -1.25 * s
    s = rng.choice([-1.0, 1.0], (N, 8, C)) * 2.0 ** -30
    x[:, :, 8, :, 0] = 1.125 * s
    x[:, :, 9, :, 0] = -1.25 * s
    x[:, :, 2, :, 0] = 2.0 ** -28
    x[:, :, 10, :, 0] = 2.0 ** -28
    for r in range(N):
        at = [0, C - 1, int(rng.integers(C)), int(rng.integers(C))]
        for g, j in zip(rng.permutation(8)[:4], at): x[r, g, 0, j, 0] = 2.0 ** 30 * rng.choice([-1.0, 1.0])
    u = d["u"].astype(np.float32).reshape(N, 128, 128, 4)
    u[:, :, ::16] = 0
    w = np.zeros((N, 128, 4, 128, 4), np.float32)
    for h in range(0, 128, 16):
        u[:, h, h, 0] = 1.125 * k
        u[:, h + 1, h, 0] = k
        w[:, h + 8, 0, h, 0] = 0.5
        w[:, h + 9, 0, h + 1, 0] = 0.5
        w[:, h + 10, 0, h + 2, 0] = 32.0
        w[:, h + 10, 0, h + 10, 0] = 32.0
    return {"x": x.reshape(N, 128, 4 * C).astype(BF), "u": u.reshape(N, 128, 512).astype(BF), "v": d["v"], **stored(trees(rng)), **weights(rng, w.astype(BF))}
def setup_inputs_odd(rng):
    d = numbers_of(rng)
    x = (1.0 + (2 * rng.integers(0, 64, (N, 16, 8, C, 4)) + 1) * 2.0 ** -7) * np.exp2(-rng.integers(0, 7, (N, 16, 8, C, 4)).astype(np.float64)) * rng.choice([-1.0, 1.0], (N, 16, 8, C, 4))
    x[:, :, 0, :, 0] = 1.96875 * 2.0 ** 8 * rng.choice([-1.0, 1.0], (N, 16, C))
    e = rng.choice([-1.0, 1.0], (N, 8, C)) * 2.0 ** -5
    x[:, ::2, 1, :, 0] = 1.125 * e
    x[:, ::2, 2, :, 0] = -e
    u = d["u"].reshape(N, 128, 128, 4)
    u[:, :, ::16] = 0
    for h in range(0, 128, 16): u[:, h + 1:h + 3, h, 0] = 1
    return {"x": x.astype(np.float32).reshape(N, 128, 4 * C).astype(BF), "u": u.reshape(N, 128, 512), "v": d["v"], **stored(trees(rng)), **layers(rng, [0, 8])}
def setup_inputs_ends(rng):
    d = numbers_of(rng)
    o, e = rng.permutation(N) % 4, rng.permutation(N) % 4
    x = np.zeros((N, 128, C, 4))
    u = d["u"].astype(np.float32).reshape(N, 128, 128, 4)
    v = d["v"].astype(np.float32)
    w = np.zeros((N, 128, 4, 128, 4), np.float32)
    t = np.zeros((N, 8, C), np.int64)
    i = np.arange(128)
    last = i % 16 == 15
    for r in range(N):
        h = rng.permutation(8)
        c = np.where(h < 2, 0.0, h % 2 * 2.0 - 1.0)[None, :, None]
        a = -(0.9 + 0.1 * rng.random((128, C, 4))) * 2.0 ** 30
        if o[r] == 1: a = a * rng.choice([-1.0, 1.0], (C, 1))
        if o[r] == 2: a = -(1.0 + 0.125 * rng.integers(0, 8, (128, C, 4))) * 2.0 ** -30
        if o[r] == 3: a = d["x"][r].astype(np.float32).reshape(128, C, 4)[:, :1]
        x[r] = a
        if o[r] < 2:
            x[r, last] = 2.0 ** -30
            u[r, :, ::16] = c * (0.9 + 0.1 * rng.random((128, 8, 4))) * 2.0 ** 30
            v[r] = rng.choice([-1.0, 1.0], (128, 512)) * (0.9 + 0.1 * rng.random((128, 512))) * 2.0 ** 30
        if o[r] == 2:
            u[r, :, ::16] = c * (1.0 + 0.125 * rng.integers(0, 8, (128, 8, 4))) * 2.0 ** -30
            v[r] = rng.choice([-1.0, 1.0], (128, 512)) * (1.0 + 0.125 * rng.integers(0, 8, (128, 512))) * 2.0 ** -30
        if o[r] == 3: u[r, :, ::16] *= np.abs(c).astype(np.float32)
        k = np.where(last, [32.0, 32.0, 256.0, 2.0 ** -8][o[r]], 32.0)
        for b in range(4): w[r, i, b, i, b] = k
        for g in range(8):
            if e[r] == 0: t[r, g] = grown(lean(0, g % 2), np.arange(C))
            if e[r] == 1: t[r, g] = grown(lean(1, g % 2), np.concatenate([[0], np.arange(C - 1, 0, -1)]))
            if e[r] >= 2: t[r, g] = grown(ragged(rng, GAPS[g - 6]) if g >= 6 else full(rng, 128 if e[r] == 2 else (C - 125) // 3), shuffled(rng))
    return {"x": x.astype(np.float32).reshape(N, 128, 4 * C).astype(BF), "u": u.reshape(N, 128, 512).astype(BF), "v": v.astype(BF), **stored(t), **weights(rng, w.astype(BF))}
def setup_inputs_spread(rng):
    d = setup_inputs(rng)
    d["x"] = wide(rng, N, 128, 4 * C, cols=6)
    return d
def check_inputs(d):
    b = []
    for k in ("x", "u", "v"):
        a = np.abs(d[k].astype(np.float32))
        if not (np.isfinite(a).all() and ((a == 0) | (a >= 2.0 ** -30) & (a <= 2.0 ** 30)).all()): b.append("a value of " + k)
    e = np.stack([gentries(d["se"][r]) for r in range(N)])
    if not ((e >= 0) & (e < 2 * C)).all(): b.append("an entry of se")
    else:
        if e[:, :, 0].any(): b.append("se: entry 0")
        if (np.diff(np.sort(e[:, :, 1:], axis=2), axis=2) == 0).any(): b.append("se: equal seats")
        a = e >> 1
        for n in range(7): a = np.take_along_axis(e >> 1, a, 2)
        if a.any(): b.append("se: a place from which eight steps don't lead to place 0")
    none, least, most = [emit(mx_ref.quantize(np.full((128, 16), k, np.float32).astype(BF)))[1][0, 0] for k in (0.0, 2.0 ** -8, 2.0 ** 8)]
    for r in range(N):
        if ((d["wc"][r] == 0x7F) | (d["wc"][r] == 0xFF)).any(): b.append("wc: a code that is no number")
        s = mx_ref.live(d["ws"][r])
        if ((s != none) & ((s < least) | (s > most))).any(): b.append("ws: a scale out of range")
        if (((d["wc"][r].reshape(16, 8, 512, 4) & 0x7F) != 0) & (s == none)[:, None, :, None]).any(): b.append("wc: a code other than zero under the scale of zeros")
    return b
def reference(x, u, v, se, wc, ws):
    qu = [mx_ref.quantize(u[r]) for r in range(N)]
    lay = [pk(wc[r], ws[r]) for r in range(N)]
    seat = [gentries(se[r]).astype(np.int64) for r in range(N)]
    par = [seat[r] >> 1 for r in range(N)]
    now = [x[r] for r in range(N)]
    y, im = np.zeros((N, 128, C), np.float32), np.zeros((N, 8, C), np.float32)
    oc, osc = np.zeros((N, 128, 4 * C), np.uint8), np.zeros((N, 16, C), np.uint8)
    for step in STEP:
        q = [mx_ref.quantize(now[r]) for r in range(N)]
        layered, child = [], []
        for r in range(N):
            layered.append(tile([mx_ref.matmul(pick(lay[r], np.arange(128 * b, 128 * b + 128)), q[r]) * np.float32(0.03125) for b in range(4)]))
            turn = (mx_ref.matmul(qu[r], q[r])[::16] < 0).astype(np.int64)
            seat[r] = seat[r] ^ np.take_along_axis(turn, par[r], 1)
            c = np.full((8, 2 * C), -1, np.int64)
            np.put_along_axis(c, seat[r][:, 1:], np.tile(np.arange(1, C), (8, 1)), 1)
            child.append(c)
        for r in range(N):
            p = r ^ step
            m = np.zeros((8, C), np.int64)
            for depth in range(8):
                at = np.take_along_axis(m, par[r], 1)
                c = np.take_along_axis(child[p], 2 * at + (seat[r] & 1), 1)
                m = np.where(c < 0, at, c)
                m[:, 0] = 0
            e = mx_ref.quantize(gcols(layered[p], m))
            above = gcols(decode(q[r]).astype(BF), par[r]).astype(np.float32)
            now[r] = ((decode(e) + above) * np.float32(0.5)).astype(BF)
            im[r] = m
    for r in range(N):
        z = mx_ref.quantize(now[r])
        y[r] = mx_ref.matmul(mx_ref.quantize(v[r]), z)
        oc[r], osc[r] = emit(z)
    return {"y": y, "im": im, "oc": oc, "osc": osc}

@@ -1,0 +1,451 @@
+from concourse.bass import IndirectOffsetOnAxis
+from concourse.mybir import dt, AluOpType, AxisListType, ActivationFunctionType
+
+N, C, R = 8, 288, 3
+STEP = [2, 4, 1]
+A, F = AluOpType, ActivationFunctionType
+BF, F32, I32, U16, FP8, U8 = "bfloat16", "float32", "int32", "uint16", "float8_e4m3fn_x4", "uint8"
+
+
+def _sb(n, d):
+    return ("sbuf", [128, n], d)
+
+
+SCRATCH = {
+    "xin": _sb(4 * C, BF), "uin": _sb(512, BF), "vin": _sb(512, BF), "sei": _sb(18, I32),
+    "wq": _sb(512, FP8), "wp": _sb(512, U8),
+    "uq": _sb(128, FP8), "up": _sb(128, U8), "ur": _sb(128, FP8), "urp": _sb(128, U8),
+    "vq": _sb(128, FP8), "vp": _sb(128, U8), "eq": _sb(512, FP8), "ep": _sb(512, U8),
+    "xq": _sb(4 * C, FP8), "xp": _sb(4 * C, U8), "hq": _sb(R * C, FP8), "hp": _sb(R * C, U8),
+    "lq": _sb(R * C, FP8), "lp": _sb(R * C, U8),
+    "half": _sb(512, BF), "et": _sb(2048, BF), "xt": _sb(R * 4 * C, BF), "ht": _sb(R * 4 * C, BF),
+    "fb": _sb(R * 4 * C, BF), "fp": _sb(R * 4 * C, BF), "db": _sb(R * 4 * C, BF),
+    "pi": _sb(1, I32), "qi": _sb(1, I32), "gi": _sb(1, I32), "qf": _sb(1, F32),
+    "bi": _sb(4, I32), "li": _sb(4, I32), "bf": _sb(4, F32), "lf": _sb(4, F32), "bc": _sb(4, F32),
+    "ca": _sb(4, F32), "cb": _sb(4, F32), "cc": _sb(4, F32), "ini": _sb(4, F32),
+    "t16": _sb(C, BF), "ij": _sb(C, BF), "mask": _sb(C, BF), "mask2": _sb(128, BF), "rst": _sb(C, BF),
+    "pm": _sb(2, F32), "c2": _sb(2, F32), "lui": _sb(8, I32), "lu": _sb(8, U16), "addi": _sb(18, I32),
+    "alt": _sb(592, BF), "om1": _sb(C, BF),
+    "sea": _sb(18, I32), "seu": _sb(18, U16), "pari": _sb(18, I32), "paru": _sb(18, U16),
+    "ch": _sb(592, BF), "loff": _sb(40, U16), "gm": _sb(64, F32), "red": _sb(6, F32),
+    "gl": _sb(224, BF), "gs": _sb(224, BF), "v0": _sb(512, BF), "ol": _sb(18, U16),
+    "top": _sb(16, F32), "sg": _sb(C, BF), "pr": _sb(C, BF), "a2r": _sb(C, BF),
+    "a2m": _sb(C, BF), "a2s": _sb(C, BF), "a4m": _sb(C, BF), "a4s": _sb(C, BF),
+    "an2": _sb(18, U16), "an4": _sb(18, U16), "om2": _sb(C, BF), "om4": _sb(C, BF), "om8": _sb(C, BF),
+    "tau": _sb(R * C, BF), "ox": _sb((R + 1) * 272, BF), "sc": _sb(R * 272, BF), "ks": _sb(R * 32, BF),
+    "kl": _sb(R * 32, BF), "k8": _sb(R * 16, BF), "ku": _sb(R * 32, U16),
+    "w": _sb((R + 1) * C, BF), "k2": _sb(R * C, BF), "k4": _sb(R * C, BF), "kk": _sb(R * C, BF),
+    "z1": _sb(R * C, BF), "z2": _sb(R * C, BF), "z4": _sb(R * C, BF), "on1": _sb(C, BF), "on2": _sb(C, BF), "on4": _sb(C, BF),
+    "km": _sb(R * C, BF), "kc": _sb(R * C, BF), "kap": _sb(R * 18, U16),
+    "vp0": _sb(512, BF), "vp1": _sb(512, BF), "vp2": _sb(512, BF), "v1": _sb(R * 512, BF),
+    "mm": _sb(R * C, BF), "ms": _sb(R * C, BF), "mo": _sb(R * 18, U16),
+    "ims": _sb(C, F32), "ys": _sb(C, F32),
+    "dv": ("dram", [128, 32], BF), "dl1": ("dram", [128, 32], BF), "dl2": ("dram", [128, 32], BF),
+    "dt1": ("dram", [8, 512], BF), "dt2": ("dram", [8, 512], BF),
+    "ps": ("psum", [128, 4096], F32),
+}
+NDMA = 24
+SEMAPHORES = (["cv", "cs", "ct", "cg", "loc", "va", "vb1", "vb2"] + ["ha%d" % r for r in range(R)]
+              + ["ka%d" % r for r in range(R)] + ["d%d" % i for i in range(NDMA)])
+
+
+def tracker(g, T):
+    qs = {"v": g.vector, "s": g.scalar, "t": g.tensor, "g": g, "y": g.sync}
+    own = {"v": "cv", "s": "cs", "t": "ct", "g": "cg"}
+    total, waited = {}, {q: {} for q in qs}
+    wrote, read = {}, {}
+    nd = [0]
+
+    def wait(q, sem, val):
+        if waited[q].get(sem, 0) < val:
+            qs[q].wait_ge(T.sem[sem], val)
+            waited[q][sem] = val
+
+    def before(q, reads, writes):
+        need = {}
+        for k in list(reads) + list(writes):
+            if k in wrote:
+                s, v = wrote[k]
+                need[s] = max(need.get(s, 0), v)
+        for k in writes:
+            for s, v in read.get(k, []):
+                need[s] = max(need.get(s, 0), v)
+        for s in sorted(need):
+            wait(q, s, need[s])
+
+    def after(reads, writes, mark):
+        for k in writes:
+            wrote[k] = mark
+            read[k] = []
+        for k in reads:
+            if k not in writes:
+                read.setdefault(k, []).append(mark)
+
+    def op(q, fn, reads, writes):
+        before(q, reads, writes)
+        s = own[q]
+        total[s] = total.get(s, 0) + 1
+        fn(qs[q]).then_inc(T.sem[s], 1)
+        after(reads, writes, (s, total[s]))
+
+    def dma(q, fn, reads, writes):
+        before(q, reads, writes)
+        s = "d%d" % nd[0]
+        nd[0] += 1
+        total[s] = 16
+        fn(qs[q]).then_inc(T.sem[s], 16)
+        after(reads, writes, (s, 16))
+
+    def send(fn, reads, count):
+        before("g", reads, [])
+        fn()
+        total["loc"] = total.get("loc", 0) + count
+
+    def arrive(sem, val, keys):
+        total[sem] = val
+        for k in keys:
+            wrote[k] = (sem, val)
+            read[k] = []
+
+    def finish():
+        for s in sorted(total):
+            if max(waited[q].get(s, 0) for q in qs) < total[s]:
+                wait("g", s, total[s])
+
+    return op, dma, send, arrive, finish
+
+
+def rank_program(g, core, T, topo):
+    rank = T.rank_of(core)
+    if rank is None:
+        return
+    op, dma, send, arrive, finish = tracker(g, T)
+    mate = [T.cores[rank ^ s] for s in STEP]
+
+    def remote(r, dst, src, sem):
+        d = mate[r]
+        rid, pid = topo.addr(d, core)
+        g.remote_dma(dst, src, T.sem[sem], T.sem.loc, pid, rid, topo.mask(core, d))
+
+    def eng(r):
+        return len(topo.engines(core, mate[r]))
+
+    def ts(out, in0, s1, s2, o0, o1, reads, writes):
+        if s2 is None:
+            op("v", lambda q: q.tensor_scalar(out, in0, s1, None, o0), reads, writes)
+        else:
+            op("v", lambda q: q.tensor_scalar(out, in0, s1, s2, o0, o1), reads, writes)
+
+    def tt(out, a, b, o, reads, writes):
+        op("v", lambda q: q.tensor_tensor(out, a, b, o), reads, writes)
+
+    def cp(out, in_, reads, writes):
+        op("v", lambda q: q.tensor_copy(out, in_), reads, writes)
+
+    def fill(ap, c, writes):
+        op("v", lambda q: q.memset(ap, c), [], writes)
+
+    def act(out, in_, reads, writes, **kw):
+        op("s", lambda q: q.activation(out, in_, F.Copy, **kw), reads, writes)
+
+    def scan(out, d1, n, reads, writes, init=0.0):
+        op("v", lambda q: q.tensor_tensor_scan(out, T.rst[:, 0:n], d1, init, A.mult, A.add), ["rst"] + reads, writes)
+
+    def mm(bank, w, wp, a, x, xp, b, reads):
+        op("t", lambda q: q.matmul_mx(T.ps[:, 512 * bank:512 * bank + C], w[:, a:a + 128], wp[:, a:a + 128],
+                                      x[:, b:b + C], xp[:, b:b + C], True, True), reads, ["b%d" % bank])
+
+    def psum(bank):
+        return T.ps[:, 512 * bank:512 * bank + C]
+
+    dma("y", lambda q: q.dma_start(T.sei[:, :], T.se[:, :]), [], ["sei"])
+    dma("s", lambda q: q.dma_start(T.xin[:, :], T.x[:, :]), [], ["xin"])
+    dma("y", lambda q: q.dma_start(T.uin[:, :], T.u[:, :]), [], ["uin"])
+    dma("s", lambda q: q.dma_start(T.wq[:, :].bitcast(dt.uint8), T.wc[:, :]), [], ["wq"])
+    dma("y", lambda q: q.dma_start(T.wp[:, :], T.ws[:, :]), [], ["wp"])
+    dma("y", lambda q: q.dma_start(T.vin[:, :], T.v[:, :]), [], ["vin"])
+
+    op("g", lambda q: q.iota(T.pi[:, :], [[0, 1]], 0, 1), [], ["pi"])
+    op("g", lambda q: q.iota(T.lui[:, :], [[16, 8]], 0, 0), [], ["lui"])
+    op("g", lambda q: q.iota(T.ij[:, :], [[1, C]], -144, 0, allow_small_or_imprecise_dtypes=True), [], ["ij"])
+    op("g", lambda q: q.iota(T.t16[:, :], [[0, 18], [1, 16]], 0, 0, allow_small_or_imprecise_dtypes=True), [], ["t16"])
+    fill(T.half[:, :], 0.5, ["half"])
+    fill(T.addi[:, :], 0, ["addi"])
+    ts(T.qi[:, :], T.pi[:, :], 15, None, A.bitwise_and, None, ["pi"], ["qi"])
+    for d in range(4):
+        ts(T.bi[:, d:d + 1], T.pi[:, :], d, 1, A.arith_shift_right, A.bitwise_and, ["pi"], ["bi"])
+    cp(T.qf[:, :], T.qi[:, :], ["qi"], ["qf"])
+    cp(T.bf[:, :], T.bi[:, :], ["bi"], ["bf"])
+    ts(T.addi[:, 0:1], T.qi[:, :], 0, 576, A.is_equal, A.mult, ["qi"], ["addi"])
+    ts(T.bc[:, :], T.bf[:, :], 288.0, None, A.add, None, ["bf"], ["bc"])
+    cp(T.loff[:, 0:1], T.bf[:, 0:1], ["bf"], ["lo1"])
+    cp(T.lu[:, :], T.lui[:, :], ["lui"], ["lu"])
+    cp(T.ch[:, 0:2 * C:2], T.ij[:, :], ["ij"], ["ch"])
+    cp(T.ch[:, 1:2 * C:2], T.ij[:, :], ["ij"], ["ch"])
+    fill(T.c2[:, 0:1], 288.0, ["c2"])
+    fill(T.c2[:, 1:2], 289.0, ["c2"])
+    ts(T.mask2[:, :], T.t16[:, 0:128], T.qf[:, 0:1], 2.0, A.is_equal, A.mult, ["t16", "qf"], ["mask2"])
+    ts(T.rst[:, :], T.t16[:, :], 0.0, None, A.not_equal, None, ["t16"], ["rst"])
+    fill(T.rst[:, 0:1], 1.0, ["rst"])
+    fill(T.v0[:, 0:1], 0.0, ["v0i"])
+    fill(T.v0[:, 1:2], -144.0, ["v0j"])
+
+    tt(T.sea[:, :], T.sei[:, :], T.addi[:, :], A.add, ["sei", "addi"], ["sea"])
+    ts(T.pari[:, :], T.sei[:, :], 1, None, A.arith_shift_right, None, ["sei"], ["pari"])
+    cp(T.seu[:, :], T.sea[:, :], ["sea"], ["seu"])
+    cp(T.paru[:, :], T.pari[:, :], ["pari"], ["paru"])
+    cp(T.ch[:, 0:592].indirect(T.seu[:, 0:18]), T.ij[:, :], ["seu", "ij"], ["ch"])
+
+    def quant(src, a, q_, p_, c, n, reads, writes):
+        op("v", lambda q: q.quantize_mx(q_[:, c:c + n], p_[:, c:c + n], src[:, a:a + 4 * n]), reads, writes)
+
+    quant(T.xin, 0, T.xq, T.xp, 0, C, ["xin"], ["xq0"])
+    quant(T.uin, 0, T.uq, T.up, 0, 128, ["uin"], ["uq"])
+    cp(T.ur[:, :].bitcast(dt.uint32), T.uq[:, 0:128].bitcast(dt.uint32).indirect(T.lu[:, 0:8]), ["uq", "lu"], ["ur"])
+    act(T.urp[:, :], T.up[:, 0:128].indirect(T.lu[:, 0:8]), ["uq", "lu"], ["urp"])
+    for b in range(4):
+        op("g", lambda q: q.affine_select(T.et[:, 512 * b:512 * b + 512], T.half[:, :], [[1, 512]], A.is_equal, 0.0, -b, -4),
+           ["half"], ["et%d" % b])
+
+    def h_tile(r):
+        for b in range(4):
+            act(T.ht[:, 4 * C * r + b:4 * C * (r + 1):4], psum(1 + b), ["b%d" % (1 + b)], ["ht%d%d" % (r, b)], scale=0.03125)
+
+    def h_quant(r):
+        quant(T.ht, 4 * C * r, T.hq, T.hp, C * r, C, ["ht%d%d" % (r, b) for b in range(4)], ["hq%d" % r])
+
+    def h_send(r):
+        n, a, b = eng(r), C * r, C * r + C
+        send(lambda: remote(r, T.lq[:, a:b].bitcast(dt.uint8), T.hq[:, a:b].bitcast(dt.uint8), "ha%d" % r), ["hq%d" % r], n)
+        send(lambda: remote(r, T.lp[:, a:b], T.hp[:, a:b], "ha%d" % r), ["hq%d" % r], n)
+        arrive("ha%d" % r, 2 * n, ["lq%d" % r])
+
+    def signs(r):
+        mm(0, T.ur, T.urp, 0, T.xq, T.xp, C * r, ["ur", "urp", "xq%d" % r])
+
+    def tau(r):
+        ts(T.tau[:, C * r:C * r + C], psum(0), 0.0, 0.5, A.is_ge, A.subtract, ["b0"], ["tau%d" % r])
+
+    def window(r):
+        return T.tau[:, C * r:C * r + C]
+
+    def key_part(r):
+        o, s, k = 272 * r, 272 * r, 32 * r
+        ox, sc, ks = "ox%d" % (r + 1), "sc%d" % r, "ks%d" % r
+        tt(T.ox[:, o + 272:o + 544], window(r).indirect(T.ol[:, 0:17]), T.ox[:, o:o + 272], A.mult,
+           ["tau%d" % r, "ol", "ox%d" % r], [ox])
+        scan(T.sc[:, s:s + 272], T.ox[:, o + 272:o + 544], 272, [ox, "ini"], [sc], T.ini[:, r:r + 1])
+        ts(T.ks[:, k + 2:k + 4], T.pm[:, :], T.sc[:, s + 31:s + 32], T.sc[:, s + 271:s + 272], A.mult, A.add, [sc, "pm"], [ks + "b"])
+        cp(T.ks[:, k:k + 2], T.sc[:, s + 15:s + 272:256], [sc], [ks + "a"])
+        for n, x, y in [(2, ["b"], "c"), (4, ["c0", "c1"], "d")]:
+            v, x = T.sc[:, s + 16 * n + 15:s + 32 * n:16], [sc] + [ks + z for z in x]
+            tt(T.ks[:, k + 2 * n:k + 3 * n], T.ks[:, k + n:k + 2 * n], v, A.subtract, x, [ks + y + "0"])
+            tt(T.ks[:, k + 3 * n:k + 4 * n], T.ks[:, k + n:k + 2 * n], v, A.add, x, [ks + y + "1"])
+            if n == 2:
+                cp(T.ks[:, k + 16:k + 24], T.sc[:, s + 143:s + 256:16], [sc], [ks + "e"])
+        return [ks + z for z in ("a", "b", "c0", "c1", "d0", "d1", "e")]
+
+    def key_send(r, keys):
+        n = eng(r)
+        send(lambda: remote(r, T.kl[:, 32 * r:32 * r + 24], T.ks[:, 32 * r:32 * r + 24], "ka%d" % r), keys, n)
+        arrive("ka%d" % r, n, ["kl%d" % r])
+
+    def f_products(r):
+        for b in range(4):
+            mm([5, 6, 7, 0][b], T.eq, T.ep, 128 * b, T.xq, T.xp, C * r, ["eq", "xq%d" % r])
+
+    def f_copies(r):
+        for b in range(4):
+            k, a = [5, 6, 7, 0][b], 4 * C * r + C * b
+            act(T.fb[:, a:a + C], psum(k), ["b%d" % k], ["fb%d%d" % (r, b)])
+
+    def f_picks(r):
+        for b in range(4):
+            a = 4 * C * r + C * b
+            act(T.fp[:, a:a + C], T.fb[:, a:a + C].indirect(T.paru[:, 0:18]), ["fb%d%d" % (r, b), "paru"], ["fp%d%d" % (r, b)])
+
+    def own_keys(r):
+        a, b, f = C * r, C * r + C, 0.5 ** (r + 1)
+        w1, k2, k4, kk, km, kc = ["%s%d" % (z, r) for z in ("w1", "k2", "k4", "kk", "km", "kc")]
+        wn, wo = "w_%d" % (r + 1), "w_%d" % r
+        W = T.w[:, b:b + C]
+        tt(W, window(r).indirect(T.paru[:, 0:18]), T.w[:, a:b], A.mult, ["tau%d" % r, "paru", wo], [wn])
+        for src, x, c, lst, dst, y in ((W, wn, T.z1, "paru", T.k2, k2), (T.k2[:, a:b], k2, T.z2, "an2", T.k4, k4),
+                                       (T.k4[:, a:b], k4, T.z4, "an4", T.kk, kk)):
+            cp(c[:, a:b], src, [x], [x + "t"])
+            tt(dst[:, a:b], src.indirect(T[lst][:, 0:18]), c[:, a:b], A.add, [x, x + "t", lst], [y])
+        tt(T.km[:, a:b], T.kk[:, a:b], T.mask[:, :], A.mult, [kk, "mask"], [km])
+        scan(T.kc[:, a:b], T.km[:, a:b], C, [km], [kc])
+        ts(T.kap[:, 18 * r:18 * r + 18], T.kc[:, a + 15:b:16], 1.0 / f, 256.0, A.mult, A.add, [kc], ["kap%d" % r])
+
+    def mapping(r, vp, vkey):
+        k, f, a, b = 32 * r, 0.5 ** (r + 1), C * r, C * r + C
+        kl, k8 = "kl%d" % r, "k8%d" % r
+        L, U = T.kl, T.ku
+        tt(T.k8[:, 16 * r:16 * r + 8], L[:, k + 8:k + 16], L[:, k + 16:k + 24], A.subtract, [kl], [k8 + "a"])
+        tt(T.k8[:, 16 * r + 8:16 * r + 16], L[:, k + 8:k + 16], L[:, k + 16:k + 24], A.add, [kl], [k8 + "b"])
+        ts(U[:, k:k + 16], L[:, k:k + 16], 1.0 / f, 256.0, A.mult, A.add, [kl], ["ku%da" % r])
+        ts(U[:, k + 16:k + 32], T.k8[:, 16 * r:16 * r + 16], 1.0 / f, 256.0, A.mult, A.add, [k8 + "a", k8 + "b"], ["ku%db" % r])
+        v1 = T.v1[:, 512 * r:512 * r + 512]
+        cp(v1.indirect(U[:, k:k + 32]), vp[:, 0:512], ["ku%da" % r, "ku%db" % r, vkey], ["v1%d" % r])
+        kap = T.kap[:, 18 * r:18 * r + 18]
+        tt(T.mm[:, a:b], v1.indirect(kap), T.mask[:, :], A.mult, ["v1%d" % r, "kap%d" % r, "mask"], ["mm%d" % r])
+        scan(T.ms[:, a:b], T.mm[:, a:b], C, ["mm%d" % r], ["ms%d" % r])
+        ts(T.mo[:, 18 * r:18 * r + 18], T.ms[:, a + 15:b:16], 144.0, None, A.add, None, ["ms%d" % r], ["mo%d" % r])
+
+    def unpack(r):
+        for b in range(4):
+            mm(1 + b, T.eq, T.ep, 128 * b, T.lq, T.lp, C * r, ["eq", "lq%d" % r])
+        for b in range(4):
+            a = 4 * C * r + C * b
+            act(T.db[:, a:a + C], psum(1 + b), ["b%d" % (1 + b)], ["db%d%d" % (r, b)])
+
+    def new_state(r):
+        for b in range(4):
+            a = 4 * C * r + C * b
+            tt(T.xt[:, 4 * C * r + b:4 * C * (r + 1):4], T.db[:, a:a + C].indirect(T.mo[:, 18 * r:18 * r + 18]), T.fp[:, a:a + C],
+               A.add, ["db%d%d" % (r, b), "mo%d" % r, "fp%d%d" % (r, b)], ["xt%d%d" % (r, b)])
+        quant(T.xt, 4 * C * r, T.xq, T.xp, C * (r + 1), C, ["xt%d%d" % (r, b) for b in range(4)], ["xq%d" % (r + 1)])
+
+    for b in range(4):
+        mm(1 + b, T.wq, T.wp, 128 * b, T.xq, T.xp, 0, ["wq", "wp", "xq0"])
+    signs(0)
+    LO = {1: 0, 2: 2, 3: 4, 4: 6, 5: 8, 6: 10, 7: 14, 8: 22}
+
+    def child(t):
+        n = max(1, 2 ** t // 16)
+        return T.ch[:, 0:2 * C].indirect(T.loff[:, LO[t]:LO[t] + n])
+
+    def level(t):
+        n = max(16, 2 ** t)
+        key = "v0s" if t < 5 else "v0%d" % t
+        act(T.v0[:, 2 ** t:2 ** t + n], child(t), ["ch", "lo%d" % t], [key])
+        if t == 8:
+            return
+        if t < 5:
+            gm, red = T.gm[:, 16 * t - 16:16 * t], T.red[:, t - 1:t]
+            tt(gm, child(t), T.mask2[:, 0:16], A.mult, ["ch", "lo%d" % t, "mask2"], ["gm%d" % t])
+            op("v", lambda q: q.tensor_reduce(red, gm, AxisListType.X, A.add), ["gm%d" % t], ["red%d" % t])
+            if t < 4:
+                ts(T.loff[:, LO[t + 1]:LO[t + 1] + 1], red, T.bc[:, t:t + 1], None, A.add, None, ["red%d" % t, "bc"], ["lo%d" % (t + 1)])
+            else:
+                ts(T.loff[:, 8:10], T.c2[:, :], red, None, A.add, None, ["red4", "c2"], ["lo5"])
+                ts(T.ol[:, 1:2], red, 0.5, 144.0, A.mult, A.add, ["red4"], ["ol"])
+            return
+        o, w = n - 32, n // 16
+        tt(T.gl[:, o:o + n], child(t), T.mask2[:, 0:n], A.mult, ["ch", "lo%d" % t, "mask2"], ["gl%d" % t])
+        scan(T.gs[:, o:o + n], T.gl[:, o:o + n], n, ["gl%d" % t], ["gs%d" % t])
+        e = T.gs[:, o + 15:o + n:16]
+        b = LO[t + 1]
+        ts(T.loff[:, b:b + w], e, 288.0, None, A.add, None, ["gs%d" % t], ["lo%d" % (t + 1)])
+        ts(T.loff[:, b + w:b + 2 * w], e, 289.0, None, A.add, None, ["gs%d" % t], ["lo%d" % (t + 1)])
+        ts(T.ol[:, w:2 * w], e, 0.5, 144.0, A.mult, A.add, ["gs%d" % t], ["ol"])
+
+    h_tile(0)
+    for t in range(1, 5):
+        level(t)
+    h_quant(0)
+    h_send(0)
+    for t in range(5, 9):
+        level(t)
+    tau(0)
+    tt(T.top[:, :], T.v0[:, 0:16], T.mask2[:, 0:16], A.mult, ["v0i", "v0j", "v0s", "mask2"], ["top"])
+    op("v", lambda q: q.tensor_reduce(T.red[:, 4:5], T.top[:, :], AxisListType.X, A.add), ["top"], ["red5"])
+    ts(T.ol[:, 0:1], T.red[:, 4:5], 0.5, 144.0, A.mult, A.add, ["red5"], ["ol"])
+    ts(T.ol[:, 16:17], T.red[:, 4:5], 0.5, 144.0, A.mult, A.add, ["red5"], ["ol"])
+    fill(T.pm[:, 0:1], -1.0, ["pm"])
+    fill(T.pm[:, 1:2], 1.0, ["pm"])
+    fill(T.ox[:, 0:1], 0.0, ["ox0"])
+    fill(T.ox[:, 256:257], 0.0, ["ox0"])
+    for r in range(R):
+        ts(T.ini[:, r:r + 1], T.qf[:, :], 0.0, -256.0 * 0.5 ** (r + 1), A.is_equal, A.mult, ["qf"], ["ini"])
+    for d in range(4):
+        ts(T.li[:, d:d + 1], T.pi[:, :], 2 ** d - 1, None, A.bitwise_and, None, ["pi"], ["li%d" % d])
+        ts(T.cb[:, d:d + 1], T.bf[:, d:d + 1], 2.0 ** (8 - d), 2.0 ** (7 - d), A.mult, A.subtract, ["bf"], ["cb%d" % d])
+    for d in range(4):
+        ts(T.ca[:, d:d + 1], T.li[:, d:d + 1], 2.0 ** d, None, A.add, None, ["li%d" % d], ["ca%d" % d])
+        ts(T.cc[:, d:d + 1], T.qf[:, :], 2.0 ** (d + 1), T.cb[:, d:d + 1], A.is_ge, A.mult, ["qf", "cb%d" % d], ["cc%d" % d])
+    for d in range(4):
+        for c, z in ((0, "cc"), (256, "cb")):
+            ts(T.ox[:, c + 2 ** d:c + 2 ** (d + 1)], T.t16[:, 2 ** d:2 ** (d + 1)], T.ca[:, d:d + 1], T[z][:, d:d + 1],
+               A.is_equal, A.mult, ["t16", "ca%d" % d, z + "%d" % d], ["ox0"])
+        ts(T.ox[:, 16 * 2 ** d:32 * 2 ** d], T.t16[:, 0:16 * 2 ** d], T.qf[:, 0:1], 2.0 ** (3 - d), A.is_equal, A.mult,
+           ["t16", "qf"], ["ox0"])
+    key_send(0, key_part(0))
+    V0 = ["v0i", "v0j", "v0s", "v05", "v06", "v07", "v08"]
+    send(lambda: remote(0, T.vp0[:, :], T.v0[:, :], "va"), V0, eng(0))
+    arrive("va", eng(0), ["vp0"])
+    dma("y", lambda q: q.dma_start(T.dv[:, :], T.v0[0:128:16, 0:512]), V0, ["dv"])
+    quant(T.et, 0, T.eq, T.ep, 0, 512, ["et%d" % b for b in range(4)], ["eq"])
+    f_products(0)
+    P18 = T.paru[:, 0:18]
+    act(T.pr[:, :], T.ij[:, 0:C].indirect(P18), ["ij", "paru"], ["pr"])
+    act(T.a2r[:, :], T.pr[:, 0:C].indirect(P18), ["pr", "paru"], ["a2r"])
+    ts(T.mask[:, :], T.t16[:, :], T.qf[:, 0:1], None, A.is_equal, None, ["t16", "qf"], ["mask"])
+    fill(T.alt[:, 0:576:2], -256.0, ["alt"])
+    fill(T.alt[:, 1:576:2], 256.0, ["alt"])
+    fill(T.alt[:, 576:592], 0.0, ["alt"])
+    fill(T.om1[:, :], 0.5, ["om1"])
+    fill(T.om1[:, 0:1], 1.0, ["om1"])
+    fill(T.on1[:, :], 0.5, ["on1"])
+    fill(T.on1[:, 0:1], 1.0, ["on1"])
+    act(T.sg[:, :], T.alt[:, 0:592].indirect(T.seu[:, 0:18]), ["alt", "seu"], ["sg"])
+    f_copies(0)
+    f_picks(0)
+    tt(T.a2m[:, :], T.pr[:, 0:C].indirect(P18), T.mask[:, :], A.mult, ["pr", "paru", "mask"], ["a2m"])
+    scan(T.a2s[:, :], T.a2m[:, :], C, ["a2m"], ["a2s"])
+    tt(T.om2[:, :], T.om1[:, 0:C].indirect(P18), T.on1[:, :], A.mult, ["om1", "on1", "paru"], ["om2"])
+    act(T.on2[:, :], T.om2[:, :], ["om2"], ["on2"])
+    ts(T.an2[:, :], T.a2s[:, 15:C:16], 144.0, None, A.add, None, ["a2s"], ["an2"])
+    tt(T.a4m[:, :], T.a2r[:, 0:C].indirect(T.an2[:, 0:18]), T.mask[:, :], A.mult, ["a2r", "an2", "mask"], ["a4m"])
+    scan(T.a4s[:, :], T.a4m[:, :], C, ["a4m"], ["a4s"])
+    tt(T.om4[:, :], T.om2[:, 0:C].indirect(T.an2[:, 0:18]), T.on2[:, :], A.mult, ["om2", "on2", "an2"], ["om4"])
+    cp(T.on4[:, :], T.om4[:, :], ["om4"], ["on4"])
+    ts(T.an4[:, :], T.a4s[:, 15:C:16], 144.0, None, A.add, None, ["a4s"], ["an4"])
+    tt(T.om8[:, :], T.om4[:, 0:C].indirect(T.an4[:, 0:18]), T.on4[:, :], A.mult, ["om4", "on4", "an4"], ["om8"])
+    tt(T.w[:, 0:C], T.om8[:, :], T.sg[:, :], A.mult, ["om8", "sg"], ["w_0"])
+    own_keys(0)
+    for r in (1, 2):
+        send(lambda: remote(r, T["dl%d" % r][:, :], T.dv[:, :], "vb%d" % r), ["dv"], eng(r))
+        arrive("vb%d" % r, eng(r), ["dl%d" % r])
+        dma("y", lambda q: q.dma_start(T["dt%d" % r][:, :], T["dl%d" % r][:, :]), ["dl%d" % r], ["dt%d" % r])
+    unpack(0)
+    mapping(0, T.vp0, "vp0")
+    ts(T.gi[:, :], T.pi[:, :], 4, None, A.arith_shift_right, None, ["pi"], ["gi"])
+    for r in (1, 2):
+        dma("g", lambda q: q.indirect_dma_start(T["vp%d" % r][:, :], None, T["dt%d" % r][:], IndirectOffsetOnAxis(ap=T.gi[:, 0:1], axis=0),
+                                                bounds_check=7), ["gi", "dt%d" % r], ["vp%d" % r])
+    new_state(0)
+
+    for r in (1, 2):
+        signs(r)
+        for b in range(4):
+            mm(1 + b, T.wq, T.wp, 128 * b, T.xq, T.xp, C * r, ["wq", "wp", "xq%d" % r])
+        tau(r)
+        h_tile(r)
+        keys = key_part(r)
+        key_send(r, keys)
+        h_quant(r)
+        h_send(r)
+        f_products(r)
+        f_copies(r)
+        f_picks(r)
+        own_keys(r)
+        if r == 1:
+            quant(T.vin, 0, T.vq, T.vp, 0, 128, ["vin"], ["vq"])
+        unpack(r)
+        mapping(r, T["vp%d" % r], "vp%d" % r)
+        if r == R - 1:
+            op("s", lambda q: q.activation(T.ims[:, :], T.v1[:, 512 * r:512 * r + 512].indirect(T.kap[:, 18 * r:18 * r + 18]),
+                                           F.Identity, bias=144.0), ["v1%d" % r, "kap%d" % r], ["ims"])
+            dma("y", lambda q: q.dma_start(T.im[:, :], T.ims[0:128:16, :]), ["ims"], [])
+        new_state(r)
+
+    a, b = R * C, R * C + C
+    mm(5, T.vq, T.vp, 0, T.xq, T.xp, a, ["vq", "xq%d" % R])
+    dma("y", lambda q: q.dma_start(T.oc[:, :], T.xq[:, a:b].bitcast(dt.uint8)), ["xq%d" % R], [])
+    for k in range(4):
+        dma("y" if k < 2 else "s", lambda q: q.dma_start(T.osc[4 * k:4 * k + 4, :], T.xp[32 * k:32 * k + 4, a:b]), ["xq%d" % R], [])
+    act(T.ys[:, :], psum(5), ["b5"], ["ys"])
+    dma("s", lambda q: q.dma_start(T.y[:, :], T.ys[:, :]), ["ys"], [])
+    finish()

@@ -20,24 +20,20 @@ SCRATCH = {
     "lq": _sb(R * C, FP8), "lp": _sb(R * C, U8),
     "half": _sb(512, BF), "et": _sb(2048, BF), "xt": _sb(R * 4 * C, BF), "ht": _sb(R * 4 * C, BF),
     "fb": _sb(R * 4 * C, BF), "fp": _sb(R * 4 * C, BF), "db": _sb(R * 4 * C, BF),
-    "pi": _sb(1, I32), "qi": _sb(1, I32), "gi": _sb(1, I32), "qf": _sb(1, F32),
-    "bi": _sb(4, I32), "li": _sb(4, I32), "bf": _sb(4, F32), "lf": _sb(4, F32), "bc": _sb(4, F32),
-    "ca": _sb(4, F32), "cb": _sb(4, F32), "cc": _sb(4, F32), "ini": _sb(4, F32),
-    "t16": _sb(C, BF), "ij": _sb(C, BF), "mask": _sb(C, BF), "mask2": _sb(128, BF), "rst": _sb(C, BF),
-    "pm": _sb(2, F32), "c2": _sb(2, F32), "lui": _sb(8, I32), "lu": _sb(8, U16), "addi": _sb(18, I32),
-    "alt": _sb(592, BF), "om1": _sb(C, BF),
-    "sea": _sb(18, I32), "seu": _sb(18, U16), "pari": _sb(18, I32), "paru": _sb(18, U16),
-    "ch": _sb(592, BF), "loff": _sb(40, U16), "gm": _sb(64, F32), "red": _sb(6, F32),
-    "gl": _sb(224, BF), "gs": _sb(224, BF), "v0": _sb(512, BF), "ol": _sb(18, U16),
-    "top": _sb(16, F32), "sg": _sb(C, BF), "pr": _sb(C, BF), "a2r": _sb(C, BF),
-    "a2m": _sb(C, BF), "a2s": _sb(C, BF), "a4m": _sb(C, BF), "a4s": _sb(C, BF),
-    "an2": _sb(18, U16), "an4": _sb(18, U16), "om2": _sb(C, BF), "om4": _sb(C, BF), "om8": _sb(C, BF),
+    "pi": _sb(1, I32), "qi": _sb(1, I32), "gi": _sb(1, I32), "qf": _sb(1, F32), "ad": _sb(1, F32),
+    "bi": _sb(4, I32), "bf": _sb(4, F32), "bc": _sb(4, F32),
+    "cl": _sb(4, F32), "cb": _sb(4, F32), "cc": _sb(4, F32), "ini": _sb(1, F32),
+    "t16": _sb(C, BF), "ij": _sb(C, BF), "ix": _sb(512, BF), "mask": _sb(C, BF), "mask2": _sb(256, BF), "rst": _sb(C, BF),
+    "pm": _sb(2, F32), "c2": _sb(2, F32), "icx": _sb(32, F32), "icy": _sb(32, F32), "lui": _sb(8, I32), "lu": _sb(8, U16),
+    "seu": _sb(18, U16), "paru": _sb(18, U16),
+    "ch": _sb(4 * C, F32), "cw": _sb(4 * C, BF), "loff": _sb(40, U16), "gm": _sb(64, F32), "red": _sb(6, F32),
+    "gl": _sb(480, F32), "gs": _sb(480, F32), "v0f": _sb(32, F32), "v0": _sb(512, BF), "ol": _sb(18, U16),
+    "top": _sb(16, F32), "pv": _sb(32, F32), "pf": _sb(16, F32), "pg": _sb(16, F32),
+    "n1": _sb(32, F32), "n2": _sb(32, F32), "n3": _sb(32, F32), "n4": _sb(32, F32), "nu": _sb(32, U16),
+    "now": _sb(800, BF), "nm": _sb(C, BF), "ns": _sb(C, BF), "no": _sb(18, U16),
     "tau": _sb(R * C, BF), "ox": _sb((R + 1) * 272, BF), "sc": _sb(R * 272, BF), "ks": _sb(R * 32, BF),
-    "kl": _sb(R * 32, BF), "k8": _sb(R * 16, BF), "ku": _sb(R * 32, U16),
-    "w": _sb((R + 1) * C, BF), "k2": _sb(R * C, BF), "k4": _sb(R * C, BF), "kk": _sb(R * C, BF),
-    "z1": _sb(R * C, BF), "z2": _sb(R * C, BF), "z4": _sb(R * C, BF), "on1": _sb(C, BF), "on2": _sb(C, BF), "on4": _sb(C, BF),
-    "km": _sb(R * C, BF), "kc": _sb(R * C, BF), "kap": _sb(R * 18, U16),
-    "vp0": _sb(512, BF), "vp1": _sb(512, BF), "vp2": _sb(512, BF), "v1": _sb(R * 512, BF),
+    "kl": _sb(R * 32, BF), "k8": _sb(R * 16, BF), "ku": _sb(R * 32, U16), "k9": _sb(R * 16, BF), "kv": _sb(R * 32, U16),
+    "vp0": _sb(512, BF), "vp1": _sb(512, BF), "vp2": _sb(512, BF), "v1": _sb(R * 512, BF), "v2": _sb(R * 512, BF),
     "mm": _sb(R * C, BF), "ms": _sb(R * C, BF), "mo": _sb(R * 18, U16),
     "ims": _sb(C, F32), "ys": _sb(C, F32),
     "dv": ("dram", [128, 32], BF), "dl1": ("dram", [128, 32], BF), "dl2": ("dram", [128, 32], BF),
@@ -145,11 +141,14 @@ def rank_program(g, core, T, topo):
     def fill(ap, c, writes):
         op("v", lambda q: q.memset(ap, c), [], writes)
 
-    def act(out, in_, reads, writes, **kw):
-        op("s", lambda q: q.activation(out, in_, F.Copy, **kw), reads, writes)
+    def act(out, in_, reads, writes, func=F.Copy, **kw):
+        op("s", lambda q: q.activation(out, in_, func, **kw), reads, writes)
+
+    def iota(out, pattern, base, cm, writes):
+        op("g", lambda q: q.iota(out, pattern, base, cm, allow_small_or_imprecise_dtypes=True), [], writes)
 
     def scan(out, d1, n, reads, writes, init=0.0):
-        op("v", lambda q: q.tensor_tensor_scan(out, T.rst[:, 0:n], d1, init, A.mult, A.add), ["rst"] + reads, writes)
+        op("v", lambda q: q.tensor_tensor_scan(out, T.rst[:, 0:n], d1, init, A.mult, A.add), ["rst0", "rst1"] + reads, writes)
 
     def mm(bank, w, wp, a, x, xp, b, reads):
         op("t", lambda q: q.matmul_mx(T.ps[:, 512 * bank:512 * bank + C], w[:, a:a + 128], wp[:, a:a + 128],
@@ -158,54 +157,18 @@ def rank_program(g, core, T, topo):
     def psum(bank):
         return T.ps[:, 512 * bank:512 * bank + C]
 
-    dma("y", lambda q: q.dma_start(T.sei[:, :], T.se[:, :]), [], ["sei"])
-    dma("s", lambda q: q.dma_start(T.xin[:, :], T.x[:, :]), [], ["xin"])
-    dma("y", lambda q: q.dma_start(T.uin[:, :], T.u[:, :]), [], ["uin"])
-    dma("s", lambda q: q.dma_start(T.wq[:, :].bitcast(dt.uint8), T.wc[:, :]), [], ["wq"])
-    dma("y", lambda q: q.dma_start(T.wp[:, :], T.ws[:, :]), [], ["wp"])
-    dma("y", lambda q: q.dma_start(T.vin[:, :], T.v[:, :]), [], ["vin"])
-
-    op("g", lambda q: q.iota(T.pi[:, :], [[0, 1]], 0, 1), [], ["pi"])
-    op("g", lambda q: q.iota(T.lui[:, :], [[16, 8]], 0, 0), [], ["lui"])
-    op("g", lambda q: q.iota(T.ij[:, :], [[1, C]], -144, 0, allow_small_or_imprecise_dtypes=True), [], ["ij"])
-    op("g", lambda q: q.iota(T.t16[:, :], [[0, 18], [1, 16]], 0, 0, allow_small_or_imprecise_dtypes=True), [], ["t16"])
-    fill(T.half[:, :], 0.5, ["half"])
-    fill(T.addi[:, :], 0, ["addi"])
-    ts(T.qi[:, :], T.pi[:, :], 15, None, A.bitwise_and, None, ["pi"], ["qi"])
-    for d in range(4):
-        ts(T.bi[:, d:d + 1], T.pi[:, :], d, 1, A.arith_shift_right, A.bitwise_and, ["pi"], ["bi"])
-    cp(T.qf[:, :], T.qi[:, :], ["qi"], ["qf"])
-    cp(T.bf[:, :], T.bi[:, :], ["bi"], ["bf"])
-    ts(T.addi[:, 0:1], T.qi[:, :], 0, 576, A.is_equal, A.mult, ["qi"], ["addi"])
-    ts(T.bc[:, :], T.bf[:, :], 288.0, None, A.add, None, ["bf"], ["bc"])
-    cp(T.loff[:, 0:1], T.bf[:, 0:1], ["bf"], ["lo1"])
-    cp(T.lu[:, :], T.lui[:, :], ["lui"], ["lu"])
-    cp(T.ch[:, 0:2 * C:2], T.ij[:, :], ["ij"], ["ch"])
-    cp(T.ch[:, 1:2 * C:2], T.ij[:, :], ["ij"], ["ch"])
-    fill(T.c2[:, 0:1], 288.0, ["c2"])
-    fill(T.c2[:, 1:2], 289.0, ["c2"])
-    ts(T.mask2[:, :], T.t16[:, 0:128], T.qf[:, 0:1], 2.0, A.is_equal, A.mult, ["t16", "qf"], ["mask2"])
-    ts(T.rst[:, :], T.t16[:, :], 0.0, None, A.not_equal, None, ["t16"], ["rst"])
-    fill(T.rst[:, 0:1], 1.0, ["rst"])
-    fill(T.v0[:, 0:1], 0.0, ["v0i"])
-    fill(T.v0[:, 1:2], -144.0, ["v0j"])
-
-    tt(T.sea[:, :], T.sei[:, :], T.addi[:, :], A.add, ["sei", "addi"], ["sea"])
-    ts(T.pari[:, :], T.sei[:, :], 1, None, A.arith_shift_right, None, ["sei"], ["pari"])
-    cp(T.seu[:, :], T.sea[:, :], ["sea"], ["seu"])
-    cp(T.paru[:, :], T.pari[:, :], ["pari"], ["paru"])
-    cp(T.ch[:, 0:592].indirect(T.seu[:, 0:18]), T.ij[:, :], ["seu", "ij"], ["ch"])
-
     def quant(src, a, q_, p_, c, n, reads, writes):
         op("v", lambda q: q.quantize_mx(q_[:, c:c + n], p_[:, c:c + n], src[:, a:a + 4 * n]), reads, writes)
 
-    quant(T.xin, 0, T.xq, T.xp, 0, C, ["xin"], ["xq0"])
-    quant(T.uin, 0, T.uq, T.up, 0, 128, ["uin"], ["uq"])
-    cp(T.ur[:, :].bitcast(dt.uint32), T.uq[:, 0:128].bitcast(dt.uint32).indirect(T.lu[:, 0:8]), ["uq", "lu"], ["ur"])
-    act(T.urp[:, :], T.up[:, 0:128].indirect(T.lu[:, 0:8]), ["uq", "lu"], ["urp"])
-    for b in range(4):
-        op("g", lambda q: q.affine_select(T.et[:, 512 * b:512 * b + 512], T.half[:, :], [[1, 512]], A.is_equal, 0.0, -b, -4),
-           ["half"], ["et%d" % b])
+    def signs(r):
+        mm(0, T.ur, T.urp, 0, T.xq, T.xp, C * r, ["ur", "urp", "xq%d" % r])
+
+    def h_products(r):
+        for b in range(4):
+            mm(1 + b, T.wq, T.wp, 128 * b, T.xq, T.xp, C * r, ["wq", "wp", "xq%d" % r])
+
+    def tau(r):
+        act(T.tau[:, C * r:C * r + C], psum(0), ["b0"], ["tau%d" % r], F.Sign, bias=2.0 ** -100)
 
     def h_tile(r):
         for b in range(4):
@@ -220,21 +183,12 @@ def rank_program(g, core, T, topo):
         send(lambda: remote(r, T.lp[:, a:b], T.hp[:, a:b], "ha%d" % r), ["hq%d" % r], n)
         arrive("ha%d" % r, 2 * n, ["lq%d" % r])
 
-    def signs(r):
-        mm(0, T.ur, T.urp, 0, T.xq, T.xp, C * r, ["ur", "urp", "xq%d" % r])
-
-    def tau(r):
-        ts(T.tau[:, C * r:C * r + C], psum(0), 0.0, 0.5, A.is_ge, A.subtract, ["b0"], ["tau%d" % r])
-
-    def window(r):
-        return T.tau[:, C * r:C * r + C]
-
     def key_part(r):
         o, s, k = 272 * r, 272 * r, 32 * r
         ox, sc, ks = "ox%d" % (r + 1), "sc%d" % r, "ks%d" % r
-        tt(T.ox[:, o + 272:o + 544], window(r).indirect(T.ol[:, 0:17]), T.ox[:, o:o + 272], A.mult,
-           ["tau%d" % r, "ol", "ox%d" % r], [ox])
-        scan(T.sc[:, s:s + 272], T.ox[:, o + 272:o + 544], 272, [ox, "ini"], [sc], T.ini[:, r:r + 1])
+        tt(T.ox[:, o + 272:o + 544], T.tau[:, C * r:C * r + C].indirect(T.ol[:, 0:17]), T.ox[:, o:o + 272], A.mult,
+           ["tau%d" % r, "ol0", "ol1"] + (OX if r == 0 else ["ox%d" % r]), [ox])
+        scan(T.sc[:, s:s + 272], T.ox[:, o + 272:o + 544], 272, [ox, "ini"], [sc], T.ini[:, 0:1])
         ts(T.ks[:, k + 2:k + 4], T.pm[:, :], T.sc[:, s + 31:s + 32], T.sc[:, s + 271:s + 272], A.mult, A.add, [sc, "pm"], [ks + "b"])
         cp(T.ks[:, k:k + 2], T.sc[:, s + 15:s + 272:256], [sc], [ks + "a"])
         for n, x, y in [(2, ["b"], "c"), (4, ["c0", "c1"], "d")]:
@@ -243,12 +197,22 @@ def rank_program(g, core, T, topo):
             tt(T.ks[:, k + 3 * n:k + 4 * n], T.ks[:, k + n:k + 2 * n], v, A.add, x, [ks + y + "1"])
             if n == 2:
                 cp(T.ks[:, k + 16:k + 24], T.sc[:, s + 143:s + 256:16], [sc], [ks + "e"])
-        return [ks + z for z in ("a", "b", "c0", "c1", "d0", "d1", "e")]
 
-    def key_send(r, keys):
+    def key_send(r):
         n = eng(r)
-        send(lambda: remote(r, T.kl[:, 32 * r:32 * r + 24], T.ks[:, 32 * r:32 * r + 24], "ka%d" % r), keys, n)
+        send(lambda: remote(r, T.kl[:, 32 * r:32 * r + 24], T.ks[:, 32 * r:32 * r + 24], "ka%d" % r),
+             ["ks%d%s" % (r, z) for z in ("a", "b", "c0", "c1", "d0", "d1", "e")], n)
         arrive("ka%d" % r, n, ["kl%d" % r])
+
+    def key_list(r, src, last, lst, deps, out):
+        k, e = 32 * r, 16 * r
+        tt(last[:, e:e + 8], src[:, k + 8:k + 16], src[:, k + 16:k + 24], A.subtract, deps, [out + "x"])
+        tt(last[:, e + 8:e + 16], src[:, k + 8:k + 16], src[:, k + 16:k + 24], A.add, deps, [out + "y"])
+        ts(lst[:, k:k + 16], src[:, k:k + 16], 256.0, None, A.add, None, deps, [out + "a"])
+        ts(lst[:, k + 16:k + 32], last[:, e:e + 16], 256.0, None, A.add, None, [out + "x", out + "y"], [out + "b"])
+
+    def own_list(r):
+        key_list(r, T.ks, T.k9, T.kv, ["ks%d%s" % (r, z) for z in ("a", "b", "c0", "c1", "d0", "d1", "e")], "kv%d" % r)
 
     def f_products(r):
         for b in range(4):
@@ -264,34 +228,15 @@ def rank_program(g, core, T, topo):
             a = 4 * C * r + C * b
             act(T.fp[:, a:a + C], T.fb[:, a:a + C].indirect(T.paru[:, 0:18]), ["fb%d%d" % (r, b), "paru"], ["fp%d%d" % (r, b)])
 
-    def own_keys(r):
-        a, b, f = C * r, C * r + C, 0.5 ** (r + 1)
-        w1, k2, k4, kk, km, kc = ["%s%d" % (z, r) for z in ("w1", "k2", "k4", "kk", "km", "kc")]
-        wn, wo = "w_%d" % (r + 1), "w_%d" % r
-        W = T.w[:, b:b + C]
-        tt(W, window(r).indirect(T.paru[:, 0:18]), T.w[:, a:b], A.mult, ["tau%d" % r, "paru", wo], [wn])
-        for src, x, c, lst, dst, y in ((W, wn, T.z1, "paru", T.k2, k2), (T.k2[:, a:b], k2, T.z2, "an2", T.k4, k4),
-                                       (T.k4[:, a:b], k4, T.z4, "an4", T.kk, kk)):
-            cp(c[:, a:b], src, [x], [x + "t"])
-            tt(dst[:, a:b], src.indirect(T[lst][:, 0:18]), c[:, a:b], A.add, [x, x + "t", lst], [y])
-        tt(T.km[:, a:b], T.kk[:, a:b], T.mask[:, :], A.mult, [kk, "mask"], [km])
-        scan(T.kc[:, a:b], T.km[:, a:b], C, [km], [kc])
-        ts(T.kap[:, 18 * r:18 * r + 18], T.kc[:, a + 15:b:16], 1.0 / f, 256.0, A.mult, A.add, [kc], ["kap%d" % r])
-
-    def mapping(r, vp, vkey):
-        k, f, a, b = 32 * r, 0.5 ** (r + 1), C * r, C * r + C
-        kl, k8 = "kl%d" % r, "k8%d" % r
-        L, U = T.kl, T.ku
-        tt(T.k8[:, 16 * r:16 * r + 8], L[:, k + 8:k + 16], L[:, k + 16:k + 24], A.subtract, [kl], [k8 + "a"])
-        tt(T.k8[:, 16 * r + 8:16 * r + 16], L[:, k + 8:k + 16], L[:, k + 16:k + 24], A.add, [kl], [k8 + "b"])
-        ts(U[:, k:k + 16], L[:, k:k + 16], 1.0 / f, 256.0, A.mult, A.add, [kl], ["ku%da" % r])
-        ts(U[:, k + 16:k + 32], T.k8[:, 16 * r:16 * r + 16], 1.0 / f, 256.0, A.mult, A.add, [k8 + "a", k8 + "b"], ["ku%db" % r])
-        v1 = T.v1[:, 512 * r:512 * r + 512]
-        cp(v1.indirect(U[:, k:k + 32]), vp[:, 0:512], ["ku%da" % r, "ku%db" % r, vkey], ["v1%d" % r])
-        kap = T.kap[:, 18 * r:18 * r + 18]
-        tt(T.mm[:, a:b], v1.indirect(kap), T.mask[:, :], A.mult, ["v1%d" % r, "kap%d" % r, "mask"], ["mm%d" % r])
-        scan(T.ms[:, a:b], T.mm[:, a:b], C, ["mm%d" % r], ["ms%d" % r])
-        ts(T.mo[:, 18 * r:18 * r + 18], T.ms[:, a + 15:b:16], 144.0, None, A.add, None, ["ms%d" % r], ["mo%d" % r])
+    def mapping(r):
+        k, a, b, z = 32 * r, C * r, C * r + C, "%d" % r
+        key_list(r, T.kl, T.k8, T.ku, ["kl" + z], "ku" + z)
+        v1, v2 = T.v1[:, 512 * r:512 * r + 512], T.v2[:, 512 * r:512 * r + 512]
+        cp(v1.indirect(T.ku[:, k:k + 32]), T["vp" + z][:, 0:512], ["ku" + z + "a", "ku" + z + "b", "vp" + z], ["v1" + z])
+        cp(v2, v1.indirect(T.kv[:, k:k + 32]), ["v1" + z, "kv" + z + "a", "kv" + z + "b"], ["v2" + z])
+        tt(T.mm[:, a:b], v2.indirect(T.no[:, 0:18]), T.mask[:, :], A.mult, ["v2" + z, "no", "mask"], ["mm" + z])
+        scan(T.ms[:, a:b], T.mm[:, a:b], C, ["mm" + z], ["ms" + z])
+        ts(T.mo[:, 18 * r:18 * r + 18], T.ms[:, a + 15:b:16], 144.0, None, A.add, None, ["ms" + z], ["mo" + z])
 
     def unpack(r):
         for b in range(4):
@@ -307,111 +252,207 @@ def rank_program(g, core, T, topo):
                A.add, ["db%d%d" % (r, b), "mo%d" % r, "fp%d%d" % (r, b)], ["xt%d%d" % (r, b)])
         quant(T.xt, 4 * C * r, T.xq, T.xp, C * (r + 1), C, ["xt%d%d" % (r, b) for b in range(4)], ["xq%d" % (r + 1)])
 
+    dma("y", lambda q: q.dma_start(T.sei[:, :], T.se[:, :]), [], ["sei"])
+    dma("s", lambda q: q.dma_start(T.xin[:, :], T.x[:, :]), [], ["xin"])
+    dma("y", lambda q: q.dma_start(T.uin[:, :], T.u[:, :]), [], ["uin"])
+    dma("s", lambda q: q.dma_start(T.wq[:, :].bitcast(dt.uint8), T.wc[:, :]), [], ["wq"])
+    dma("y", lambda q: q.dma_start(T.wp[:, :], T.ws[:, :]), [], ["wp"])
+    dma("y", lambda q: q.dma_start(T.vin[:, :], T.v[:, :]), [], ["vin"])
+
+    op("g", lambda q: q.iota(T.pi[:, :], [[0, 1]], 0, 1), [], ["pi"])
+    iota(T.ij[:, :], [[1, C]], -144, 0, ["ij"])
+    iota(T.t16[:, :], [[0, 18], [1, 16]], 0, 0, ["t16"])
+    iota(T.c2[:, :], [[1, 2]], 288, 0, ["c2"])
+    op("g", lambda q: q.iota(T.lui[:, :], [[16, 8]], 0, 0), [], ["lui"])
+    iota(T.pm[:, :], [[2, 2]], -1, 0, ["pm"])
+    iota(T.icx[:, :], [[16, 32]], 144, 0, ["icx"])
+    fill(T.half[:, :], 0.5, ["half"])
     for b in range(4):
-        mm(1 + b, T.wq, T.wp, 128 * b, T.xq, T.xp, 0, ["wq", "wp", "xq0"])
-    signs(0)
+        op("g", lambda q: q.affine_select(T.et[:, 512 * b:512 * b + 512], T.half[:, :], [[1, 512]], A.is_equal, 0.0, -b, -4),
+           ["half"], ["et%d" % b])
+    iota(T.ix[:, :], [[1, 512]], -256, 0, ["ix"])
+    ts(T.qi[:, :], T.pi[:, :], 15, None, A.bitwise_and, None, ["pi"], ["qi"])
+    BI = ["bi%d" % d for d in range(4)]
+    for d in range(4):
+        ts(T.bi[:, d:d + 1], T.pi[:, :], d, 1, A.arith_shift_right, A.bitwise_and, ["pi"], [BI[d]])
+    cp(T.qf[:, :], T.qi[:, :], ["qi"], ["qf"])
+    cp(T.bf[:, :], T.bi[:, :], BI, ["bf"])
+    ts(T.ad[:, :], T.qf[:, :], 0.0, 576.0, A.is_equal, A.mult, ["qf"], ["ad"])
+    for i in range(2):
+        ts(T.ch[:, i:2 * C:2], T.ij[:, :], 288.0, None, A.add, None, ["ij"], ["ch%d" % i])
+        cp(T.cw[:, i:2 * C:2], T.ij[:, :], ["ij"], ["cw%d" % i])
+    ts(T.bc[:, :], T.bf[:, :], 288.0, None, A.add, None, ["bf"], ["bc"])
+    cp(T.loff[:, 0:1], T.bf[:, 0:1], ["bf"], ["lo1"])
+    ts(T.mask2[:, 0:256], T.t16[:, 0:256], T.qf[:, 0:1], 2.0, A.is_equal, A.mult, ["t16", "qf"], ["mask2"])
+    ts(T.rst[:, 1:C], T.t16[:, 1:C], 0.0, None, A.not_equal, None, ["t16"], ["rst1"])
+    for d in range(4):
+        act(T.cb[:, d:d + 1], T.bf[:, d:d + 1], ["bf"], ["cb%d" % d], F.Identity, scale=2.0 ** (8 - d), bias=-2.0 ** (7 - d))
+
+    ts(T.seu[:, 0:1], T.sei[:, 0:1], T.ad[:, 0:1], None, A.add, None, ["sei", "ad"], ["seu0"])
+    cp(T.seu[:, 1:18], T.sei[:, 1:18], ["sei"], ["seu1"])
+    cp(T.lu[:, :], T.lui[:, :], ["lui"], ["lu"])
+    cp(T.ch[:, 0:592].indirect(T.seu[:, 0:18]), T.ij[:, :], ["seu0", "seu1", "ij", "ch0", "ch1"], ["ch"])
+    cp(T.cw[:, 0:592].indirect(T.seu[:, 0:18]), T.ij[:, :], ["seu0", "seu1", "ij", "cw0", "cw1"], ["cw"])
+    act(T.ch[:, 2 * C:4 * C], T.cw[:, 0:2 * C], ["cw", "ch"], ["cht"], F.Identity, bias=288.0)
+    act(T.cw[:, 2 * C:4 * C], T.cw[:, 0:2 * C], ["cw"], ["cwt"])
+
+    OX = []
+    todo = []
+
+    def later(fn, *a):
+        todo.append((fn, a))
+
+    def some(n=1):
+        for i in range(n):
+            if todo:
+                fn, a = todo.pop(0)
+                fn(*a)
+
+    def ox(fn, *a):
+        k = "ox0_%d" % len(OX)
+        OX.append(k)
+        later(fn, *(a + ([k],)))
+
+    later(fill, T.v0f[:, 0:1], 200.0, ["v0i"])
+    later(fill, T.v0f[:, 1:2], -144.0, ["v0j"])
+    later(fill, T.v0[:, 0:2], -144.0, ["v0k"])
+    later(fill, T.rst[:, 0:1], 1.0, ["rst0"])
+    later(ts, T.cl[:, 2:3], T.bf[:, 1:2], 2.0, T.bf[:, 0:1], A.mult, A.add, ["bf"], ["cl2"])
+    for d in range(3):
+        later(ts, T.cc[:, d:d + 1], T.qf[:, :], 2.0 ** (d + 1), T.cb[:, d:d + 1], A.is_ge, A.mult, ["qf", "cb%d" % d], ["cc%d" % d])
+    later(ts, T.cl[:, 3:4], T.bf[:, 2:3], 4.0, T.cl[:, 2:3], A.mult, A.add, ["bf", "cl2"], ["cl3"])
+    ox(fill, T.ox[:, 0:1], 0.0)
+    ox(fill, T.ox[:, 256:257], 0.0)
+    ox(fill, T.ox[:, 8:16], 0.0)
+    for d in range(4):
+        ox(ts, T.ox[:, 16 * 2 ** d:32 * 2 ** d], T.t16[:, 0:16 * 2 ** d], T.qf[:, 0:1], 2.0 ** (3 - d), A.is_equal, A.mult, ["t16", "qf"])
+    for c, z, m in ((0, "cc", 3), (256, "cb", 4)):
+        for d in range(m):
+            if d == 0:
+                ox(cp, T.ox[:, c + 1:c + 2], T[z][:, 0:1], [z + "0"])
+            else:
+                low = T.bf[:, 0:1] if d == 1 else T.cl[:, d:d + 1]
+                ox(ts, T.ox[:, c + 2 ** d:c + 2 ** (d + 1)], T.t16[:, 0:2 ** d], low, T[z][:, d:d + 1], A.is_equal, A.mult,
+                   ["t16", "bf" if d == 1 else "cl%d" % d, z + "%d" % d])
+    later(ts, T.ini[:, :], T.qf[:, :], 0.0, -256.0, A.is_equal, A.mult, ["qf"], ["ini"])
+    later(ts, T.paru[:, :], T.sei[:, :], 0.5, 0.25, A.mult, A.subtract, ["sei"], ["paru"])
+
     LO = {1: 0, 2: 2, 3: 4, 4: 6, 5: 8, 6: 10, 7: 14, 8: 22}
 
-    def child(t):
+    def child(t, name="ch"):
         n = max(1, 2 ** t // 16)
-        return T.ch[:, 0:2 * C].indirect(T.loff[:, LO[t]:LO[t] + n])
+        deps = [name] + ([name + "t"] if t > 1 else []) + (["lo%da" % t, "lo%db" % t] if t > 4 else ["lo%d" % t])
+        return T[name][:, 0:(4 if t > 1 else 2) * C].indirect(T.loff[:, LO[t]:LO[t] + n]), deps
 
-    def level(t):
-        n = max(16, 2 ** t)
-        key = "v0s" if t < 5 else "v0%d" % t
-        act(T.v0[:, 2 ** t:2 ** t + n], child(t), ["ch", "lo%d" % t], [key])
-        if t == 8:
-            return
+    def lanes(t):
+        kid, deps = child(t)
         if t < 5:
             gm, red = T.gm[:, 16 * t - 16:16 * t], T.red[:, t - 1:t]
-            tt(gm, child(t), T.mask2[:, 0:16], A.mult, ["ch", "lo%d" % t, "mask2"], ["gm%d" % t])
+            tt(gm, kid, T.mask2[:, 0:16], A.mult, deps + ["mask2"], ["gm%d" % t])
+            some()
             op("v", lambda q: q.tensor_reduce(red, gm, AxisListType.X, A.add), ["gm%d" % t], ["red%d" % t])
+            some()
             if t < 4:
                 ts(T.loff[:, LO[t + 1]:LO[t + 1] + 1], red, T.bc[:, t:t + 1], None, A.add, None, ["red%d" % t, "bc"], ["lo%d" % (t + 1)])
+                some()
             else:
-                ts(T.loff[:, 8:10], T.c2[:, :], red, None, A.add, None, ["red4", "c2"], ["lo5"])
-                ts(T.ol[:, 1:2], red, 0.5, 144.0, A.mult, A.add, ["red4"], ["ol"])
+                ts(T.loff[:, 8:9], red, T.c2[:, 0:1], None, A.add, None, ["red4", "c2"], ["lo5a"])
+                ts(T.loff[:, 9:10], red, T.c2[:, 1:2], None, A.add, None, ["red4", "c2"], ["lo5b"])
+                ts(T.pv[:, 1:2], red, 0.5, None, A.mult, None, ["red4"], ["pv4"])
             return
+        n = 2 ** t
         o, w = n - 32, n // 16
-        tt(T.gl[:, o:o + n], child(t), T.mask2[:, 0:n], A.mult, ["ch", "lo%d" % t, "mask2"], ["gl%d" % t])
+        tt(T.gl[:, o:o + n], kid, T.mask2[:, 0:n], A.mult, deps + ["mask2"], ["gl%d" % t])
+        some()
         scan(T.gs[:, o:o + n], T.gl[:, o:o + n], n, ["gl%d" % t], ["gs%d" % t])
+        some()
         e = T.gs[:, o + 15:o + n:16]
-        b = LO[t + 1]
-        ts(T.loff[:, b:b + w], e, 288.0, None, A.add, None, ["gs%d" % t], ["lo%d" % (t + 1)])
-        ts(T.loff[:, b + w:b + 2 * w], e, 289.0, None, A.add, None, ["gs%d" % t], ["lo%d" % (t + 1)])
-        ts(T.ol[:, w:2 * w], e, 0.5, 144.0, A.mult, A.add, ["gs%d" % t], ["ol"])
+        if t < 8:
+            b = LO[t + 1]
+            ts(T.loff[:, b:b + w], e, 288.0, None, A.add, None, ["gs%d" % t], ["lo%da" % (t + 1)])
+            ts(T.loff[:, b + w:b + 2 * w], e, 289.0, None, A.add, None, ["gs%d" % t], ["lo%db" % (t + 1)])
+        ts(T.pv[:, w:2 * w], e, 0.5, None, A.mult, None, ["gs%d" % t], ["pv%d" % t])
 
+    def whole(t):
+        kid, deps = child(t, "cw")
+        n = max(16, 2 ** t)
+        act(T.v0[:, 2 ** t:2 ** t + n], kid, deps, ["v0t" if t < 5 else "v0%d" % t])
+        if t < 4:
+            kid, deps = child(t)
+            act(T.v0f[:, 2 ** t:2 ** t + 16], kid, deps, ["v0s"])
+
+    lanes(1)
+    quant(T.xin, 0, T.xq, T.xp, 0, C, ["xin"], ["xq0"])
+    h_products(0)
+    lanes(2)
+    quant(T.uin, 0, T.uq, T.up, 0, 128, ["uin"], ["uq"])
+    act(T.urp[:, :], T.up[:, 0:128].indirect(T.lu[:, 0:8]), ["uq", "lu"], ["urp"])
+    lanes(3)
+    cp(T.ur[:, :].bitcast(dt.uint32), T.uq[:, 0:128].bitcast(dt.uint32).indirect(T.lu[:, 0:8]), ["uq", "lu"], ["ur"])
+    signs(0)
     h_tile(0)
-    for t in range(1, 5):
-        level(t)
+    for t in range(1, 4):
+        whole(t)
+    lanes(4)
+    whole(4)
+    tau(0)
+    lanes(5)
+    whole(5)
+    lanes(6)
+    whole(6)
     h_quant(0)
     h_send(0)
-    for t in range(5, 9):
-        level(t)
-    tau(0)
-    tt(T.top[:, :], T.v0[:, 0:16], T.mask2[:, 0:16], A.mult, ["v0i", "v0j", "v0s", "mask2"], ["top"])
+    tt(T.top[:, :], T.v0f[:, 0:16], T.mask2[:, 0:16], A.mult, ["v0i", "v0j", "v0s", "mask2"], ["top"])
+    lanes(7)
     op("v", lambda q: q.tensor_reduce(T.red[:, 4:5], T.top[:, :], AxisListType.X, A.add), ["top"], ["red5"])
-    ts(T.ol[:, 0:1], T.red[:, 4:5], 0.5, 144.0, A.mult, A.add, ["red5"], ["ol"])
-    ts(T.ol[:, 16:17], T.red[:, 4:5], 0.5, 144.0, A.mult, A.add, ["red5"], ["ol"])
-    fill(T.pm[:, 0:1], -1.0, ["pm"])
-    fill(T.pm[:, 1:2], 1.0, ["pm"])
-    fill(T.ox[:, 0:1], 0.0, ["ox0"])
-    fill(T.ox[:, 256:257], 0.0, ["ox0"])
-    for r in range(R):
-        ts(T.ini[:, r:r + 1], T.qf[:, :], 0.0, -256.0 * 0.5 ** (r + 1), A.is_equal, A.mult, ["qf"], ["ini"])
-    for d in range(4):
-        ts(T.li[:, d:d + 1], T.pi[:, :], 2 ** d - 1, None, A.bitwise_and, None, ["pi"], ["li%d" % d])
-        ts(T.cb[:, d:d + 1], T.bf[:, d:d + 1], 2.0 ** (8 - d), 2.0 ** (7 - d), A.mult, A.subtract, ["bf"], ["cb%d" % d])
-    for d in range(4):
-        ts(T.ca[:, d:d + 1], T.li[:, d:d + 1], 2.0 ** d, None, A.add, None, ["li%d" % d], ["ca%d" % d])
-        ts(T.cc[:, d:d + 1], T.qf[:, :], 2.0 ** (d + 1), T.cb[:, d:d + 1], A.is_ge, A.mult, ["qf", "cb%d" % d], ["cc%d" % d])
-    for d in range(4):
-        for c, z in ((0, "cc"), (256, "cb")):
-            ts(T.ox[:, c + 2 ** d:c + 2 ** (d + 1)], T.t16[:, 2 ** d:2 ** (d + 1)], T.ca[:, d:d + 1], T[z][:, d:d + 1],
-               A.is_equal, A.mult, ["t16", "ca%d" % d, z + "%d" % d], ["ox0"])
-        ts(T.ox[:, 16 * 2 ** d:32 * 2 ** d], T.t16[:, 0:16 * 2 ** d], T.qf[:, 0:1], 2.0 ** (3 - d), A.is_equal, A.mult,
-           ["t16", "qf"], ["ox0"])
-    key_send(0, key_part(0))
-    V0 = ["v0i", "v0j", "v0s", "v05", "v06", "v07", "v08"]
+    some()
+    ts(T.pv[:, 0:1], T.red[:, 4:5], 0.5, None, A.mult, None, ["red5"], ["pv0"])
+    some(2)
+    PV = ["pv0", "pv4", "pv5", "pv6", "pv7"]
+    ts(T.pf[:, 0:16], T.pv[:, 0:16], 144.0, -288.0, A.is_ge, A.mult, PV, ["pf"])
+    some(2)
+    tt(T.pg[:, 0:16], T.pf[:, 0:16], T.pv[:, 0:16], A.add, PV + ["pf"], ["pg"])
+    some(2)
+    ts(T.ol[:, 0:16], T.pg[:, 0:16], 144.0, None, A.add, None, ["pg"], ["ol0"])
+    ts(T.ol[:, 16:17], T.pg[:, 0:1], 144.0, None, A.add, None, ["pg"], ["ol1"])
+    some(99)
+    whole(7)
+    whole(8)
+    key_part(0)
+    key_send(0)
+    V0 = ["v0k", "v0t", "v05", "v06", "v07", "v08"]
     send(lambda: remote(0, T.vp0[:, :], T.v0[:, :], "va"), V0, eng(0))
     arrive("va", eng(0), ["vp0"])
     dma("y", lambda q: q.dma_start(T.dv[:, :], T.v0[0:128:16, 0:512]), V0, ["dv"])
+    later(ts, T.icy[:, :], T.icx[:, :], T.qf[:, 0:1], None, A.add, None, ["icx", "qf"], ["icy"])
+    lanes(8)
     quant(T.et, 0, T.eq, T.ep, 0, 512, ["et%d" % b for b in range(4)], ["eq"])
-    f_products(0)
-    P18 = T.paru[:, 0:18]
-    act(T.pr[:, :], T.ij[:, 0:C].indirect(P18), ["ij", "paru"], ["pr"])
-    act(T.a2r[:, :], T.pr[:, 0:C].indirect(P18), ["pr", "paru"], ["a2r"])
+    PV = PV + ["pv8"]
+    ts(T.n1[:, :], T.pv[:, :], 144.0, None, A.is_ge, None, PV, ["n1"])
+    tt(T.n2[:, :], T.icy[:, :], T.pv[:, :], A.subtract, PV + ["icy"], ["n2"])
     ts(T.mask[:, :], T.t16[:, :], T.qf[:, 0:1], None, A.is_equal, None, ["t16", "qf"], ["mask"])
-    fill(T.alt[:, 0:576:2], -256.0, ["alt"])
-    fill(T.alt[:, 1:576:2], 256.0, ["alt"])
-    fill(T.alt[:, 576:592], 0.0, ["alt"])
-    fill(T.om1[:, :], 0.5, ["om1"])
-    fill(T.om1[:, 0:1], 1.0, ["om1"])
-    fill(T.on1[:, :], 0.5, ["on1"])
-    fill(T.on1[:, 0:1], 1.0, ["on1"])
-    act(T.sg[:, :], T.alt[:, 0:592].indirect(T.seu[:, 0:18]), ["alt", "seu"], ["sg"])
+    ksk = ["ks0%s" % z for z in ("a", "b", "c0", "c1", "d0", "d1", "e")]
+    tt(T.k9[:, 0:8], T.ks[:, 8:16], T.ks[:, 16:24], A.subtract, ksk, ["kv0x"])
+    tt(T.n3[:, :], T.n1[:, :], T.n2[:, :], A.mult, ["n1", "n2"], ["n3"])
+    tt(T.k9[:, 8:16], T.ks[:, 8:16], T.ks[:, 16:24], A.add, ksk, ["kv0y"])
+    tt(T.n4[:, :], T.n3[:, :], T.pv[:, :], A.add, PV + ["n3"], ["n4"])
+    ts(T.kv[:, 0:16], T.ks[:, 0:16], 256.0, None, A.add, None, ksk, ["kv0a"])
+    ts(T.nu[:, :], T.n4[:, :], 144.0, None, A.add, None, ["n4"], ["nu"])
+    ts(T.kv[:, 16:32], T.k9[:, 0:16], 256.0, None, A.add, None, ["kv0x", "kv0y"], ["kv0b"])
+    cp(T.now[:, 0:800].indirect(T.nu[:, 0:32]), T.ix[:, :], ["nu", "ix"], ["now"])
+    tt(T.nm[:, :], T.now[:, 0:C], T.mask[:, :], A.mult, ["now", "mask"], ["nm"])
+    scan(T.ns[:, :], T.nm[:, :], C, ["nm"], ["ns"])
+    ts(T.no[:, :], T.ns[:, 15:C:16], 256.0, None, A.add, None, ["ns"], ["no"])
+    f_products(0)
     f_copies(0)
     f_picks(0)
-    tt(T.a2m[:, :], T.pr[:, 0:C].indirect(P18), T.mask[:, :], A.mult, ["pr", "paru", "mask"], ["a2m"])
-    scan(T.a2s[:, :], T.a2m[:, :], C, ["a2m"], ["a2s"])
-    tt(T.om2[:, :], T.om1[:, 0:C].indirect(P18), T.on1[:, :], A.mult, ["om1", "on1", "paru"], ["om2"])
-    act(T.on2[:, :], T.om2[:, :], ["om2"], ["on2"])
-    ts(T.an2[:, :], T.a2s[:, 15:C:16], 144.0, None, A.add, None, ["a2s"], ["an2"])
-    tt(T.a4m[:, :], T.a2r[:, 0:C].indirect(T.an2[:, 0:18]), T.mask[:, :], A.mult, ["a2r", "an2", "mask"], ["a4m"])
-    scan(T.a4s[:, :], T.a4m[:, :], C, ["a4m"], ["a4s"])
-    tt(T.om4[:, :], T.om2[:, 0:C].indirect(T.an2[:, 0:18]), T.on2[:, :], A.mult, ["om2", "on2", "an2"], ["om4"])
-    cp(T.on4[:, :], T.om4[:, :], ["om4"], ["on4"])
-    ts(T.an4[:, :], T.a4s[:, 15:C:16], 144.0, None, A.add, None, ["a4s"], ["an4"])
-    tt(T.om8[:, :], T.om4[:, 0:C].indirect(T.an4[:, 0:18]), T.on4[:, :], A.mult, ["om4", "on4", "an4"], ["om8"])
-    tt(T.w[:, 0:C], T.om8[:, :], T.sg[:, :], A.mult, ["om8", "sg"], ["w_0"])
-    own_keys(0)
     for r in (1, 2):
         send(lambda: remote(r, T["dl%d" % r][:, :], T.dv[:, :], "vb%d" % r), ["dv"], eng(r))
         arrive("vb%d" % r, eng(r), ["dl%d" % r])
         dma("y", lambda q: q.dma_start(T["dt%d" % r][:, :], T["dl%d" % r][:, :]), ["dl%d" % r], ["dt%d" % r])
     unpack(0)
-    mapping(0, T.vp0, "vp0")
     ts(T.gi[:, :], T.pi[:, :], 4, None, A.arith_shift_right, None, ["pi"], ["gi"])
+    mapping(0)
     for r in (1, 2):
         dma("g", lambda q: q.indirect_dma_start(T["vp%d" % r][:, :], None, T["dt%d" % r][:], IndirectOffsetOnAxis(ap=T.gi[:, 0:1], axis=0),
                                                 bounds_check=7), ["gi", "dt%d" % r], ["vp%d" % r])
@@ -419,25 +460,23 @@ def rank_program(g, core, T, topo):
 
     for r in (1, 2):
         signs(r)
-        for b in range(4):
-            mm(1 + b, T.wq, T.wp, 128 * b, T.xq, T.xp, C * r, ["wq", "wp", "xq%d" % r])
+        h_products(r)
         tau(r)
         h_tile(r)
-        keys = key_part(r)
-        key_send(r, keys)
+        key_part(r)
+        key_send(r)
         h_quant(r)
         h_send(r)
         f_products(r)
         f_copies(r)
         f_picks(r)
-        own_keys(r)
+        own_list(r)
         if r == 1:
             quant(T.vin, 0, T.vq, T.vp, 0, 128, ["vin"], ["vq"])
         unpack(r)
-        mapping(r, T["vp%d" % r], "vp%d" % r)
+        mapping(r)
         if r == R - 1:
-            op("s", lambda q: q.activation(T.ims[:, :], T.v1[:, 512 * r:512 * r + 512].indirect(T.kap[:, 18 * r:18 * r + 18]),
-                                           F.Identity, bias=144.0), ["v1%d" % r, "kap%d" % r], ["ims"])
+            act(T.ims[:, :], T.v2[:, 512 * r:512 * r + 512].indirect(T.no[:, 0:18]), ["v2%d" % r, "no"], ["ims"], F.Identity, bias=144.0)
             dma("y", lambda q: q.dma_start(T.im[:, :], T.ims[0:128:16, :]), ["ims"], [])
         new_state(r)
 

from concourse.bass import IndirectOffsetOnAxis
from concourse.mybir import dt, AluOpType, AxisListType, ActivationFunctionType

N, C, R = 8, 288, 3
STEP = [2, 4, 1]
A, F = AluOpType, ActivationFunctionType
BF, F32, I32, U16, FP8, U8 = "bfloat16", "float32", "int32", "uint16", "float8_e4m3fn_x4", "uint8"


def _sb(n, d):
    return ("sbuf", [128, n], d)


SCRATCH = {
    "xin": _sb(4 * C, BF), "uin": _sb(512, BF), "vin": _sb(512, BF), "sei": _sb(18, I32),
    "wq": _sb(512, FP8), "wp": _sb(512, U8),
    "uq": _sb(128, FP8), "up": _sb(128, U8), "ur": _sb(128, FP8), "urp": _sb(128, U8),
    "vq": _sb(128, FP8), "vp": _sb(128, U8), "eq": _sb(512, FP8), "ep": _sb(512, U8),
    "xq": _sb(4 * C, FP8), "xp": _sb(4 * C, U8), "hq": _sb(R * C, FP8), "hp": _sb(R * C, U8),
    "lq": _sb(R * C, FP8), "lp": _sb(R * C, U8),
    "half": _sb(512, BF), "et": _sb(2048, BF), "xt": _sb(R * 4 * C, BF), "ht": _sb(R * 4 * C, BF),
    "fb": _sb(R * 4 * C, BF), "fp": _sb(R * 4 * C, BF), "db": _sb(R * 4 * C, BF),
    "pi": _sb(1, I32), "qi": _sb(1, I32), "gi": _sb(1, I32), "qf": _sb(1, F32), "ad": _sb(1, F32),
    "bi": _sb(4, I32), "bf": _sb(4, F32), "bc": _sb(4, F32),
    "cl": _sb(4, F32), "cb": _sb(4, F32), "cc": _sb(4, F32), "ini": _sb(1, F32),
    "t16": _sb(C, BF), "ij": _sb(C, BF), "ix": _sb(512, BF), "mask": _sb(C, BF), "mask2": _sb(256, BF), "rst": _sb(C, BF),
    "pm": _sb(2, F32), "c2": _sb(2, F32), "icx": _sb(32, F32), "icy": _sb(32, F32), "lui": _sb(8, I32), "lu": _sb(8, U16),
    "seu": _sb(18, U16), "paru": _sb(18, U16),
    "ch": _sb(4 * C, F32), "cw": _sb(4 * C, BF), "loff": _sb(40, U16), "gm": _sb(64, F32), "red": _sb(6, F32),
    "gl": _sb(480, F32), "gs": _sb(480, F32), "v0f": _sb(32, F32), "v0": _sb(512, BF), "ol": _sb(18, U16),
    "top": _sb(16, F32), "pv": _sb(32, F32), "pf": _sb(16, F32), "pg": _sb(16, F32),
    "n1": _sb(32, F32), "n2": _sb(32, F32), "n3": _sb(32, F32), "n4": _sb(32, F32), "nu": _sb(32, U16),
    "now": _sb(800, BF), "nm": _sb(C, BF), "ns": _sb(C, BF), "no": _sb(18, U16),
    "tau": _sb(R * C, BF), "ox": _sb((R + 1) * 272, BF), "sc": _sb(R * 272, BF), "ks": _sb(R * 32, BF),
    "kl": _sb(R * 32, BF), "k8": _sb(R * 16, BF), "ku": _sb(R * 32, U16), "k9": _sb(R * 16, BF), "kv": _sb(R * 32, U16),
    "vp0": _sb(512, BF), "vp1": _sb(512, BF), "vp2": _sb(512, BF), "v1": _sb(R * 512, BF), "v2": _sb(R * 512, BF),
    "mm": _sb(R * C, BF), "ms": _sb(R * C, BF), "mo": _sb(R * 18, U16),
    "ims": _sb(C, F32), "ys": _sb(C, F32),
    "dv": ("dram", [128, 32], BF), "dl1": ("dram", [128, 32], BF), "dl2": ("dram", [128, 32], BF),
    "dt1": ("dram", [8, 512], BF), "dt2": ("dram", [8, 512], BF),
    "ps": ("psum", [128, 4096], F32),
}
NDMA = 24
SEMAPHORES = (["cv", "cs", "ct", "cg", "loc", "va", "vb1", "vb2"] + ["ha%d" % r for r in range(R)]
              + ["ka%d" % r for r in range(R)] + ["d%d" % i for i in range(NDMA)])


def tracker(g, T):
    qs = {"v": g.vector, "s": g.scalar, "t": g.tensor, "g": g, "y": g.sync}
    own = {"v": "cv", "s": "cs", "t": "ct", "g": "cg"}
    total, waited = {}, {q: {} for q in qs}
    wrote, read = {}, {}
    nd = [0]

    def wait(q, sem, val):
        if waited[q].get(sem, 0) < val:
            qs[q].wait_ge(T.sem[sem], val)
            waited[q][sem] = val

    def before(q, reads, writes):
        need = {}
        for k in list(reads) + list(writes):
            if k in wrote:
                s, v = wrote[k]
                need[s] = max(need.get(s, 0), v)
        for k in writes:
            for s, v in read.get(k, []):
                need[s] = max(need.get(s, 0), v)
        for s in sorted(need):
            wait(q, s, need[s])

    def after(reads, writes, mark):
        for k in writes:
            wrote[k] = mark
            read[k] = []
        for k in reads:
            if k not in writes:
                read.setdefault(k, []).append(mark)

    def op(q, fn, reads, writes):
        before(q, reads, writes)
        s = own[q]
        total[s] = total.get(s, 0) + 1
        fn(qs[q]).then_inc(T.sem[s], 1)
        after(reads, writes, (s, total[s]))

    def dma(q, fn, reads, writes):
        before(q, reads, writes)
        s = "d%d" % nd[0]
        nd[0] += 1
        total[s] = 16
        fn(qs[q]).then_inc(T.sem[s], 16)
        after(reads, writes, (s, 16))

    def send(fn, reads, count):
        before("g", reads, [])
        fn()
        total["loc"] = total.get("loc", 0) + count

    def arrive(sem, val, keys):
        total[sem] = val
        for k in keys:
            wrote[k] = (sem, val)
            read[k] = []

    def finish():
        for s in sorted(total):
            if max(waited[q].get(s, 0) for q in qs) < total[s]:
                wait("g", s, total[s])

    return op, dma, send, arrive, finish


def rank_program(g, core, T, topo):
    rank = T.rank_of(core)
    if rank is None:
        return
    op, dma, send, arrive, finish = tracker(g, T)
    mate = [T.cores[rank ^ s] for s in STEP]

    def remote(r, dst, src, sem):
        d = mate[r]
        rid, pid = topo.addr(d, core)
        g.remote_dma(dst, src, T.sem[sem], T.sem.loc, pid, rid, topo.mask(core, d))

    def eng(r):
        return len(topo.engines(core, mate[r]))

    def ts(out, in0, s1, s2, o0, o1, reads, writes):
        if s2 is None:
            op("v", lambda q: q.tensor_scalar(out, in0, s1, None, o0), reads, writes)
        else:
            op("v", lambda q: q.tensor_scalar(out, in0, s1, s2, o0, o1), reads, writes)

    def tt(out, a, b, o, reads, writes):
        op("v", lambda q: q.tensor_tensor(out, a, b, o), reads, writes)

    def cp(out, in_, reads, writes):
        op("v", lambda q: q.tensor_copy(out, in_), reads, writes)

    def fill(ap, c, writes):
        op("v", lambda q: q.memset(ap, c), [], writes)

    def act(out, in_, reads, writes, func=F.Copy, **kw):
        op("s", lambda q: q.activation(out, in_, func, **kw), reads, writes)

    def iota(out, pattern, base, cm, writes):
        op("g", lambda q: q.iota(out, pattern, base, cm, allow_small_or_imprecise_dtypes=True), [], writes)

    def scan(out, d1, n, reads, writes, init=0.0):
        op("v", lambda q: q.tensor_tensor_scan(out, T.rst[:, 0:n], d1, init, A.mult, A.add), ["rst0", "rst1"] + reads, writes)

    def mm(bank, w, wp, a, x, xp, b, reads):
        op("t", lambda q: q.matmul_mx(T.ps[:, 512 * bank:512 * bank + C], w[:, a:a + 128], wp[:, a:a + 128],
                                      x[:, b:b + C], xp[:, b:b + C], True, True), reads, ["b%d" % bank])

    def psum(bank):
        return T.ps[:, 512 * bank:512 * bank + C]

    def quant(src, a, q_, p_, c, n, reads, writes):
        op("v", lambda q: q.quantize_mx(q_[:, c:c + n], p_[:, c:c + n], src[:, a:a + 4 * n]), reads, writes)

    def signs(r):
        mm(0, T.ur, T.urp, 0, T.xq, T.xp, C * r, ["ur", "urp", "xq%d" % r])

    def h_products(r):
        for b in range(4):
            mm(1 + b, T.wq, T.wp, 128 * b, T.xq, T.xp, C * r, ["wq", "wp", "xq%d" % r])

    def tau(r):
        act(T.tau[:, C * r:C * r + C], psum(0), ["b0"], ["tau%d" % r], F.Sign, bias=2.0 ** -100)

    def h_tile(r):
        for b in range(4):
            act(T.ht[:, 4 * C * r + b:4 * C * (r + 1):4], psum(1 + b), ["b%d" % (1 + b)], ["ht%d%d" % (r, b)], scale=0.03125)

    def h_quant(r):
        quant(T.ht, 4 * C * r, T.hq, T.hp, C * r, C, ["ht%d%d" % (r, b) for b in range(4)], ["hq%d" % r])

    def h_send(r):
        n, a, b = eng(r), C * r, C * r + C
        send(lambda: remote(r, T.lq[:, a:b].bitcast(dt.uint8), T.hq[:, a:b].bitcast(dt.uint8), "ha%d" % r), ["hq%d" % r], n)
        send(lambda: remote(r, T.lp[:, a:b], T.hp[:, a:b], "ha%d" % r), ["hq%d" % r], n)
        arrive("ha%d" % r, 2 * n, ["lq%d" % r])

    def key_part(r):
        o, s, k = 272 * r, 272 * r, 32 * r
        ox, sc, ks = "ox%d" % (r + 1), "sc%d" % r, "ks%d" % r
        tt(T.ox[:, o + 272:o + 544], T.tau[:, C * r:C * r + C].indirect(T.ol[:, 0:17]), T.ox[:, o:o + 272], A.mult,
           ["tau%d" % r, "ol0", "ol1"] + (OX if r == 0 else ["ox%d" % r]), [ox])
        scan(T.sc[:, s:s + 272], T.ox[:, o + 272:o + 544], 272, [ox, "ini"], [sc], T.ini[:, 0:1])
        ts(T.ks[:, k + 2:k + 4], T.pm[:, :], T.sc[:, s + 31:s + 32], T.sc[:, s + 271:s + 272], A.mult, A.add, [sc, "pm"], [ks + "b"])
        cp(T.ks[:, k:k + 2], T.sc[:, s + 15:s + 272:256], [sc], [ks + "a"])
        for n, x, y in [(2, ["b"], "c"), (4, ["c0", "c1"], "d")]:
            v, x = T.sc[:, s + 16 * n + 15:s + 32 * n:16], [sc] + [ks + z for z in x]
            tt(T.ks[:, k + 2 * n:k + 3 * n], T.ks[:, k + n:k + 2 * n], v, A.subtract, x, [ks + y + "0"])
            tt(T.ks[:, k + 3 * n:k + 4 * n], T.ks[:, k + n:k + 2 * n], v, A.add, x, [ks + y + "1"])
            if n == 2:
                cp(T.ks[:, k + 16:k + 24], T.sc[:, s + 143:s + 256:16], [sc], [ks + "e"])

    def key_send(r):
        n = eng(r)
        send(lambda: remote(r, T.kl[:, 32 * r:32 * r + 24], T.ks[:, 32 * r:32 * r + 24], "ka%d" % r),
             ["ks%d%s" % (r, z) for z in ("a", "b", "c0", "c1", "d0", "d1", "e")], n)
        arrive("ka%d" % r, n, ["kl%d" % r])

    def key_list(r, src, last, lst, deps, out):
        k, e = 32 * r, 16 * r
        tt(last[:, e:e + 8], src[:, k + 8:k + 16], src[:, k + 16:k + 24], A.subtract, deps, [out + "x"])
        tt(last[:, e + 8:e + 16], src[:, k + 8:k + 16], src[:, k + 16:k + 24], A.add, deps, [out + "y"])
        ts(lst[:, k:k + 16], src[:, k:k + 16], 256.0, None, A.add, None, deps, [out + "a"])
        ts(lst[:, k + 16:k + 32], last[:, e:e + 16], 256.0, None, A.add, None, [out + "x", out + "y"], [out + "b"])

    def own_list(r):
        key_list(r, T.ks, T.k9, T.kv, ["ks%d%s" % (r, z) for z in ("a", "b", "c0", "c1", "d0", "d1", "e")], "kv%d" % r)

    def f_products(r):
        for b in range(4):
            mm([5, 6, 7, 0][b], T.eq, T.ep, 128 * b, T.xq, T.xp, C * r, ["eq", "xq%d" % r])

    def f_copies(r):
        for b in range(4):
            k, a = [5, 6, 7, 0][b], 4 * C * r + C * b
            act(T.fb[:, a:a + C], psum(k), ["b%d" % k], ["fb%d%d" % (r, b)])

    def f_picks(r):
        for b in range(4):
            a = 4 * C * r + C * b
            act(T.fp[:, a:a + C], T.fb[:, a:a + C].indirect(T.paru[:, 0:18]), ["fb%d%d" % (r, b), "paru"], ["fp%d%d" % (r, b)])

    def mapping(r):
        k, a, b, z = 32 * r, C * r, C * r + C, "%d" % r
        key_list(r, T.kl, T.k8, T.ku, ["kl" + z], "ku" + z)
        v1, v2 = T.v1[:, 512 * r:512 * r + 512], T.v2[:, 512 * r:512 * r + 512]
        cp(v1.indirect(T.ku[:, k:k + 32]), T["vp" + z][:, 0:512], ["ku" + z + "a", "ku" + z + "b", "vp" + z], ["v1" + z])
        cp(v2, v1.indirect(T.kv[:, k:k + 32]), ["v1" + z, "kv" + z + "a", "kv" + z + "b"], ["v2" + z])
        tt(T.mm[:, a:b], v2.indirect(T.no[:, 0:18]), T.mask[:, :], A.mult, ["v2" + z, "no", "mask"], ["mm" + z])
        scan(T.ms[:, a:b], T.mm[:, a:b], C, ["mm" + z], ["ms" + z])
        ts(T.mo[:, 18 * r:18 * r + 18], T.ms[:, a + 15:b:16], 144.0, None, A.add, None, ["ms" + z], ["mo" + z])

    def unpack(r):
        for b in range(4):
            mm(1 + b, T.eq, T.ep, 128 * b, T.lq, T.lp, C * r, ["eq", "lq%d" % r])
        for b in range(4):
            a = 4 * C * r + C * b
            act(T.db[:, a:a + C], psum(1 + b), ["b%d" % (1 + b)], ["db%d%d" % (r, b)])

    def new_state(r):
        for b in range(4):
            a = 4 * C * r + C * b
            tt(T.xt[:, 4 * C * r + b:4 * C * (r + 1):4], T.db[:, a:a + C].indirect(T.mo[:, 18 * r:18 * r + 18]), T.fp[:, a:a + C],
               A.add, ["db%d%d" % (r, b), "mo%d" % r, "fp%d%d" % (r, b)], ["xt%d%d" % (r, b)])
        quant(T.xt, 4 * C * r, T.xq, T.xp, C * (r + 1), C, ["xt%d%d" % (r, b) for b in range(4)], ["xq%d" % (r + 1)])

    dma("y", lambda q: q.dma_start(T.sei[:, :], T.se[:, :]), [], ["sei"])
    dma("s", lambda q: q.dma_start(T.xin[:, :], T.x[:, :]), [], ["xin"])
    dma("y", lambda q: q.dma_start(T.uin[:, :], T.u[:, :]), [], ["uin"])
    dma("s", lambda q: q.dma_start(T.wq[:, :].bitcast(dt.uint8), T.wc[:, :]), [], ["wq"])
    dma("y", lambda q: q.dma_start(T.wp[:, :], T.ws[:, :]), [], ["wp"])
    dma("y", lambda q: q.dma_start(T.vin[:, :], T.v[:, :]), [], ["vin"])

    op("g", lambda q: q.iota(T.pi[:, :], [[0, 1]], 0, 1), [], ["pi"])
    iota(T.ij[:, :], [[1, C]], -144, 0, ["ij"])
    iota(T.t16[:, :], [[0, 18], [1, 16]], 0, 0, ["t16"])
    iota(T.c2[:, :], [[1, 2]], 288, 0, ["c2"])
    op("g", lambda q: q.iota(T.lui[:, :], [[16, 8]], 0, 0), [], ["lui"])
    iota(T.pm[:, :], [[2, 2]], -1, 0, ["pm"])
    iota(T.icx[:, :], [[16, 32]], 144, 0, ["icx"])
    fill(T.half[:, :], 0.5, ["half"])
    for b in range(4):
        op("g", lambda q: q.affine_select(T.et[:, 512 * b:512 * b + 512], T.half[:, :], [[1, 512]], A.is_equal, 0.0, -b, -4),
           ["half"], ["et%d" % b])
    iota(T.ix[:, :], [[1, 512]], -256, 0, ["ix"])
    ts(T.qi[:, :], T.pi[:, :], 15, None, A.bitwise_and, None, ["pi"], ["qi"])
    BI = ["bi%d" % d for d in range(4)]
    for d in range(4):
        ts(T.bi[:, d:d + 1], T.pi[:, :], d, 1, A.arith_shift_right, A.bitwise_and, ["pi"], [BI[d]])
    cp(T.qf[:, :], T.qi[:, :], ["qi"], ["qf"])
    cp(T.bf[:, :], T.bi[:, :], BI, ["bf"])
    ts(T.ad[:, :], T.qf[:, :], 0.0, 576.0, A.is_equal, A.mult, ["qf"], ["ad"])
    for i in range(2):
        ts(T.ch[:, i:2 * C:2], T.ij[:, :], 288.0, None, A.add, None, ["ij"], ["ch%d" % i])
        cp(T.cw[:, i:2 * C:2], T.ij[:, :], ["ij"], ["cw%d" % i])
    ts(T.bc[:, :], T.bf[:, :], 288.0, None, A.add, None, ["bf"], ["bc"])
    cp(T.loff[:, 0:1], T.bf[:, 0:1], ["bf"], ["lo1"])
    ts(T.mask2[:, 0:256], T.t16[:, 0:256], T.qf[:, 0:1], 2.0, A.is_equal, A.mult, ["t16", "qf"], ["mask2"])
    ts(T.rst[:, 1:C], T.t16[:, 1:C], 0.0, None, A.not_equal, None, ["t16"], ["rst1"])
    for d in range(4):
        act(T.cb[:, d:d + 1], T.bf[:, d:d + 1], ["bf"], ["cb%d" % d], F.Identity, scale=2.0 ** (8 - d), bias=-2.0 ** (7 - d))

    ts(T.seu[:, 0:1], T.sei[:, 0:1], T.ad[:, 0:1], None, A.add, None, ["sei", "ad"], ["seu0"])
    cp(T.seu[:, 1:18], T.sei[:, 1:18], ["sei"], ["seu1"])
    cp(T.lu[:, :], T.lui[:, :], ["lui"], ["lu"])
    cp(T.ch[:, 0:592].indirect(T.seu[:, 0:18]), T.ij[:, :], ["seu0", "seu1", "ij", "ch0", "ch1"], ["ch"])
    cp(T.cw[:, 0:592].indirect(T.seu[:, 0:18]), T.ij[:, :], ["seu0", "seu1", "ij", "cw0", "cw1"], ["cw"])
    act(T.ch[:, 2 * C:4 * C], T.cw[:, 0:2 * C], ["cw", "ch"], ["cht"], F.Identity, bias=288.0)
    act(T.cw[:, 2 * C:4 * C], T.cw[:, 0:2 * C], ["cw"], ["cwt"])

    OX = []
    todo = []

    def later(fn, *a):
        todo.append((fn, a))

    def some(n=1):
        for i in range(n):
            if todo:
                fn, a = todo.pop(0)
                fn(*a)

    def ox(fn, *a):
        k = "ox0_%d" % len(OX)
        OX.append(k)
        later(fn, *(a + ([k],)))

    later(fill, T.v0f[:, 0:1], 200.0, ["v0i"])
    later(fill, T.v0f[:, 1:2], -144.0, ["v0j"])
    later(fill, T.v0[:, 0:2], -144.0, ["v0k"])
    later(fill, T.rst[:, 0:1], 1.0, ["rst0"])
    later(ts, T.cl[:, 2:3], T.bf[:, 1:2], 2.0, T.bf[:, 0:1], A.mult, A.add, ["bf"], ["cl2"])
    for d in range(3):
        later(ts, T.cc[:, d:d + 1], T.qf[:, :], 2.0 ** (d + 1), T.cb[:, d:d + 1], A.is_ge, A.mult, ["qf", "cb%d" % d], ["cc%d" % d])
    later(ts, T.cl[:, 3:4], T.bf[:, 2:3], 4.0, T.cl[:, 2:3], A.mult, A.add, ["bf", "cl2"], ["cl3"])
    ox(fill, T.ox[:, 0:1], 0.0)
    ox(fill, T.ox[:, 256:257], 0.0)
    ox(fill, T.ox[:, 8:16], 0.0)
    for d in range(4):
        ox(ts, T.ox[:, 16 * 2 ** d:32 * 2 ** d], T.t16[:, 0:16 * 2 ** d], T.qf[:, 0:1], 2.0 ** (3 - d), A.is_equal, A.mult, ["t16", "qf"])
    for c, z, m in ((0, "cc", 3), (256, "cb", 4)):
        for d in range(m):
            if d == 0:
                ox(cp, T.ox[:, c + 1:c + 2], T[z][:, 0:1], [z + "0"])
            else:
                low = T.bf[:, 0:1] if d == 1 else T.cl[:, d:d + 1]
                ox(ts, T.ox[:, c + 2 ** d:c + 2 ** (d + 1)], T.t16[:, 0:2 ** d], low, T[z][:, d:d + 1], A.is_equal, A.mult,
                   ["t16", "bf" if d == 1 else "cl%d" % d, z + "%d" % d])
    later(ts, T.ini[:, :], T.qf[:, :], 0.0, -256.0, A.is_equal, A.mult, ["qf"], ["ini"])
    later(ts, T.paru[:, :], T.sei[:, :], 0.5, 0.25, A.mult, A.subtract, ["sei"], ["paru"])

    LO = {1: 0, 2: 2, 3: 4, 4: 6, 5: 8, 6: 10, 7: 14, 8: 22}

    def child(t, name="ch"):
        n = max(1, 2 ** t // 16)
        deps = [name] + ([name + "t"] if t > 1 else []) + (["lo%da" % t, "lo%db" % t] if t > 4 else ["lo%d" % t])
        return T[name][:, 0:(4 if t > 1 else 2) * C].indirect(T.loff[:, LO[t]:LO[t] + n]), deps

    def lanes(t):
        kid, deps = child(t)
        if t < 5:
            gm, red = T.gm[:, 16 * t - 16:16 * t], T.red[:, t - 1:t]
            tt(gm, kid, T.mask2[:, 0:16], A.mult, deps + ["mask2"], ["gm%d" % t])
            some()
            op("v", lambda q: q.tensor_reduce(red, gm, AxisListType.X, A.add), ["gm%d" % t], ["red%d" % t])
            some()
            if t < 4:
                ts(T.loff[:, LO[t + 1]:LO[t + 1] + 1], red, T.bc[:, t:t + 1], None, A.add, None, ["red%d" % t, "bc"], ["lo%d" % (t + 1)])
                some()
            else:
                ts(T.loff[:, 8:9], red, T.c2[:, 0:1], None, A.add, None, ["red4", "c2"], ["lo5a"])
                ts(T.loff[:, 9:10], red, T.c2[:, 1:2], None, A.add, None, ["red4", "c2"], ["lo5b"])
                ts(T.pv[:, 1:2], red, 0.5, None, A.mult, None, ["red4"], ["pv4"])
            return
        n = 2 ** t
        o, w = n - 32, n // 16
        tt(T.gl[:, o:o + n], kid, T.mask2[:, 0:n], A.mult, deps + ["mask2"], ["gl%d" % t])
        some()
        scan(T.gs[:, o:o + n], T.gl[:, o:o + n], n, ["gl%d" % t], ["gs%d" % t])
        some()
        e = T.gs[:, o + 15:o + n:16]
        if t < 8:
            b = LO[t + 1]
            ts(T.loff[:, b:b + w], e, 288.0, None, A.add, None, ["gs%d" % t], ["lo%da" % (t + 1)])
            ts(T.loff[:, b + w:b + 2 * w], e, 289.0, None, A.add, None, ["gs%d" % t], ["lo%db" % (t + 1)])
        ts(T.pv[:, w:2 * w], e, 0.5, None, A.mult, None, ["gs%d" % t], ["pv%d" % t])

    def whole(t):
        kid, deps = child(t, "cw")
        n = max(16, 2 ** t)
        act(T.v0[:, 2 ** t:2 ** t + n], kid, deps, ["v0t" if t < 5 else "v0%d" % t])
        if t < 4:
            kid, deps = child(t)
            act(T.v0f[:, 2 ** t:2 ** t + 16], kid, deps, ["v0s"])

    lanes(1)
    quant(T.xin, 0, T.xq, T.xp, 0, C, ["xin"], ["xq0"])
    h_products(0)
    lanes(2)
    quant(T.uin, 0, T.uq, T.up, 0, 128, ["uin"], ["uq"])
    act(T.urp[:, :], T.up[:, 0:128].indirect(T.lu[:, 0:8]), ["uq", "lu"], ["urp"])
    lanes(3)
    cp(T.ur[:, :].bitcast(dt.uint32), T.uq[:, 0:128].bitcast(dt.uint32).indirect(T.lu[:, 0:8]), ["uq", "lu"], ["ur"])
    signs(0)
    h_tile(0)
    for t in range(1, 4):
        whole(t)
    lanes(4)
    whole(4)
    tau(0)
    lanes(5)
    whole(5)
    lanes(6)
    whole(6)
    h_quant(0)
    h_send(0)
    tt(T.top[:, :], T.v0f[:, 0:16], T.mask2[:, 0:16], A.mult, ["v0i", "v0j", "v0s", "mask2"], ["top"])
    lanes(7)
    op("v", lambda q: q.tensor_reduce(T.red[:, 4:5], T.top[:, :], AxisListType.X, A.add), ["top"], ["red5"])
    some()
    ts(T.pv[:, 0:1], T.red[:, 4:5], 0.5, None, A.mult, None, ["red5"], ["pv0"])
    some(2)
    PV = ["pv0", "pv4", "pv5", "pv6", "pv7"]
    ts(T.pf[:, 0:16], T.pv[:, 0:16], 144.0, -288.0, A.is_ge, A.mult, PV, ["pf"])
    some(2)
    tt(T.pg[:, 0:16], T.pf[:, 0:16], T.pv[:, 0:16], A.add, PV + ["pf"], ["pg"])
    some(2)
    ts(T.ol[:, 0:16], T.pg[:, 0:16], 144.0, None, A.add, None, ["pg"], ["ol0"])
    ts(T.ol[:, 16:17], T.pg[:, 0:1], 144.0, None, A.add, None, ["pg"], ["ol1"])
    some(99)
    whole(7)
    whole(8)
    key_part(0)
    key_send(0)
    V0 = ["v0k", "v0t", "v05", "v06", "v07", "v08"]
    send(lambda: remote(0, T.vp0[:, :], T.v0[:, :], "va"), V0, eng(0))
    arrive("va", eng(0), ["vp0"])
    dma("y", lambda q: q.dma_start(T.dv[:, :], T.v0[0:128:16, 0:512]), V0, ["dv"])
    later(ts, T.icy[:, :], T.icx[:, :], T.qf[:, 0:1], None, A.add, None, ["icx", "qf"], ["icy"])
    lanes(8)
    quant(T.et, 0, T.eq, T.ep, 0, 512, ["et%d" % b for b in range(4)], ["eq"])
    PV = PV + ["pv8"]
    ts(T.n1[:, :], T.pv[:, :], 144.0, None, A.is_ge, None, PV, ["n1"])
    tt(T.n2[:, :], T.icy[:, :], T.pv[:, :], A.subtract, PV + ["icy"], ["n2"])
    ts(T.mask[:, :], T.t16[:, :], T.qf[:, 0:1], None, A.is_equal, None, ["t16", "qf"], ["mask"])
    ksk = ["ks0%s" % z for z in ("a", "b", "c0", "c1", "d0", "d1", "e")]
    tt(T.k9[:, 0:8], T.ks[:, 8:16], T.ks[:, 16:24], A.subtract, ksk, ["kv0x"])
    tt(T.n3[:, :], T.n1[:, :], T.n2[:, :], A.mult, ["n1", "n2"], ["n3"])
    tt(T.k9[:, 8:16], T.ks[:, 8:16], T.ks[:, 16:24], A.add, ksk, ["kv0y"])
    tt(T.n4[:, :], T.n3[:, :], T.pv[:, :], A.add, PV + ["n3"], ["n4"])
    ts(T.kv[:, 0:16], T.ks[:, 0:16], 256.0, None, A.add, None, ksk, ["kv0a"])
    ts(T.nu[:, :], T.n4[:, :], 144.0, None, A.add, None, ["n4"], ["nu"])
    ts(T.kv[:, 16:32], T.k9[:, 0:16], 256.0, None, A.add, None, ["kv0x", "kv0y"], ["kv0b"])
    cp(T.now[:, 0:800].indirect(T.nu[:, 0:32]), T.ix[:, :], ["nu", "ix"], ["now"])
    tt(T.nm[:, :], T.now[:, 0:C], T.mask[:, :], A.mult, ["now", "mask"], ["nm"])
    scan(T.ns[:, :], T.nm[:, :], C, ["nm"], ["ns"])
    ts(T.no[:, :], T.ns[:, 15:C:16], 256.0, None, A.add, None, ["ns"], ["no"])
    f_products(0)
    f_copies(0)
    f_picks(0)
    for r in (1, 2):
        send(lambda: remote(r, T["dl%d" % r][:, :], T.dv[:, :], "vb%d" % r), ["dv"], eng(r))
        arrive("vb%d" % r, eng(r), ["dl%d" % r])
        dma("y", lambda q: q.dma_start(T["dt%d" % r][:, :], T["dl%d" % r][:, :]), ["dl%d" % r], ["dt%d" % r])
    unpack(0)
    ts(T.gi[:, :], T.pi[:, :], 4, None, A.arith_shift_right, None, ["pi"], ["gi"])
    mapping(0)
    for r in (1, 2):
        dma("g", lambda q: q.indirect_dma_start(T["vp%d" % r][:, :], None, T["dt%d" % r][:], IndirectOffsetOnAxis(ap=T.gi[:, 0:1], axis=0),
                                                bounds_check=7), ["gi", "dt%d" % r], ["vp%d" % r])
    new_state(0)

    for r in (1, 2):
        signs(r)
        h_products(r)
        tau(r)
        h_tile(r)
        key_part(r)
        key_send(r)
        h_quant(r)
        h_send(r)
        f_products(r)
        f_copies(r)
        f_picks(r)
        own_list(r)
        if r == 1:
            quant(T.vin, 0, T.vq, T.vp, 0, 128, ["vin"], ["vq"])
        unpack(r)
        mapping(r)
        if r == R - 1:
            act(T.ims[:, :], T.v2[:, 512 * r:512 * r + 512].indirect(T.no[:, 0:18]), ["v2%d" % r, "no"], ["ims"], F.Identity, bias=144.0)
            dma("y", lambda q: q.dma_start(T.im[:, :], T.ims[0:128:16, :]), ["ims"], [])
        new_state(r)

    a, b = R * C, R * C + C
    mm(5, T.vq, T.vp, 0, T.xq, T.xp, a, ["vq", "xq%d" % R])
    dma("y", lambda q: q.dma_start(T.oc[:, :], T.xq[:, a:b].bitcast(dt.uint8)), ["xq%d" % R], [])
    for k in range(4):
        dma("y" if k < 2 else "s", lambda q: q.dma_start(T.osc[4 * k:4 * k + 4, :], T.xp[32 * k:32 * k + 4, a:b]), ["xq%d" % R], [])
    act(T.ys[:, :], psum(5), ["b5"], ["ys"])
    dma("s", lambda q: q.dma_start(T.y[:, :], T.ys[:, :]), ["ys"], [])
    finish()
